import numpy as np
import ml_dtypes


def mxq(x, axis, fmt="e4m3"):
    dtype, down = {"e4m3": (ml_dtypes.float8_e4m3fn, 7), "e5m2": (ml_dtypes.float8_e5m2, 14)}[fmt]
    v = np.moveaxis(np.asarray(x, np.float32).astype(ml_dtypes.bfloat16).astype(np.float64), axis, -1)
    blocks = v.reshape(v.shape[:-1] + (-1, 32))
    amax = np.abs(blocks).max(-1, keepdims=True)
    byte = np.maximum(np.where(amax > 0, np.frexp(amax)[1] - 1 + 127, 0) - down, 1)
    scale = np.exp2(byte - 127.0)
    codes = (blocks / scale).astype(np.float32).astype(dtype).astype(np.float64)
    return np.moveaxis((codes * scale).reshape(v.shape), -1, axis)


WIDE = False


def mx_kscale(k):
    if not WIDE:
        return np.ones(k)
    levels = np.array([10, -10, 5, -5, 0])
    if k % 512:
        return np.exp2(np.random.permutation(np.resize(levels, k // 32))).repeat(32)
    a = np.empty((k // 512, 16))
    for p in range(k // 512):
        a[p, :8] = np.random.permutation(np.resize(levels, 8))
        for g in range(8):
            far = levels[np.abs(levels - a[p, g]) >= 10]
            a[p, g + 8] = far[np.random.randint(len(far))]
    return np.exp2(a.ravel()).repeat(32)


def f64(x):
    return np.asarray(x).astype(np.float64)


def striped(idx):
    return np.tile(idx.reshape(-1, 16).T, (8, 1)).astype(np.uint16)


def unstriped(offs):
    return offs[:16].T.reshape(-1).astype(np.int64)


def striped8(idx):
    return np.concatenate([x.reshape(-1, 16).T for x in idx]).astype(np.uint16)


def runs(offs, k):
    lists = np.stack([offs[16 * r : 16 * r + 16].T.reshape(-1) for r in range(8)]).astype(np.int64)
    return lists[np.arange(k) % 512 // 64]


def pack_weight(w):
    k, n = w.shape
    w = f64(np.asarray(w, np.float32).astype(ml_dtypes.bfloat16)).reshape(k // 32, 32, n)
    amax = np.abs(w).max(1)
    byte = np.clip(np.where(amax > 0, np.frexp(amax)[1] - 1 + 127 - 7, 1), 1, 254)
    scaled = (w * np.exp2(127.0 - byte)[:, None, :]).reshape(k, n).astype(np.float32)
    words = np.ascontiguousarray(scaled.reshape(k // 512, 128, 4, n).transpose(0, 1, 3, 2)).astype(ml_dtypes.float8_e4m3fn).view(np.uint8)
    return words, np.ascontiguousarray(byte.astype(np.uint8).reshape(k // 512, 16, n))


def unpack_weight(words, scales):
    g, p, n, _ = words.shape
    vals = np.ascontiguousarray(words).view(ml_dtypes.float8_e4m3fn).astype(np.float64) * np.repeat(np.exp2(scales.astype(np.float64) - 127.0), 8, axis=1)[..., None]
    return vals.transpose(0, 1, 3, 2).reshape(g * 512, n)


K, T, S, N, U = 512, 2048, 512, 512, 1024


def setup_inputs():
    n = np.random.standard_normal
    s = mx_kscale(K)[:, None]
    packed_xT = pack_weight(n((K, T)) * s)
    return {
        "x_words": packed_xT[0],
        "x_scales": packed_xT[1],
        "w1": (n((K, N)) / np.sqrt(K) / s).astype(np.float32),
        "st": n((N, U)).astype(np.float32),
        "va": np.random.uniform(0.2, 2.0, (N, U)).astype(np.float32),
        "offs": striped(np.random.permutation(T)[:S]),
        "trk": striped8(np.stack([np.random.permutation(U)[:S] for _ in range(8)])),
    }


def reference(x_words, x_scales, w1, st, va, offs, trk):
    so = f64(st)[np.arange(N)[:, None], runs(trk, N)]
    po = f64(va)[np.arange(N)[:, None], runs(trk, N)]
    kg = po / (po + 0.5)
    xq = unpack_weight(x_words, x_scales)[:, unstriped(offs)]
    y = mxq(f64(w1), 0, "e4m3").T @ xq
    sn = so + kg * (y - so)
    out = f64(st).copy()
    out[np.arange(N)[:, None], runs(trk, N)] = sn
    return out

@@ -1,0 +1,134 @@
+from contextlib import ExitStack
+
+import concourse.mybir as mybir
+
+K, T, S, N, U = 512, 2048, 512, 512, 1024
+FLOPS = 2 * K * N * S
+
+F32 = mybir.dt.float32
+BF16 = mybir.dt.bfloat16
+I32 = mybir.dt.int32
+U32 = mybir.dt.uint32
+U16 = mybir.dt.uint16
+U8 = mybir.dt.uint8
+FP8X4 = mybir.dt.float8_e4m3fn_x4
+ALU = mybir.AluOpType
+ACT = mybir.ActivationFunctionType
+
+P = 128
+PACK = 4
+TILES = N // P
+
+
+def tile_picked_kalman8_none_p_kernel(tc, x_words, x_scales, w1, st, va, offs, trk, out):
+    nc = tc.nc
+    with ExitStack() as ctx:
+        keep = ctx.enter_context(tc.tile_pool(name="keep", bufs=1))
+        psum = ctx.enter_context(tc.psum_pool(name="psum", bufs=1))
+
+        st_rows = st.rearrange("(p t) u -> t p u", t=TILES)
+        va_rows = va.rearrange("(p t) u -> t p u", t=TILES)
+        out_rows = out.rearrange("(p t) u -> t p u", t=TILES)
+
+        offsets = keep.tile([P, S // 16], U16, name="offsets")
+        tracks = keep.tile([P, S // 16], U16, name="tracks")
+        all_scales = keep.tile([P, T], U8, name="all_scales", align_bytes=64)
+        all_words = keep.tile([P, T], I32, name="all_words", align_bytes=64)
+        w_raw = keep.tile([P, PACK, N], F32, name="w_raw")
+        states = [keep.tile([P, U], F32, name="states%d" % t) for t in range(TILES)]
+
+        variances = [keep.tile([P, U], F32, name="variances%d" % t) for t in range(2)]
+        late_variances = keep.tile([P, 2, U], F32, name="late_variances")
+
+        nc.vector.memset(all_scales[:].bitcast(I32), 0)
+        nc.sync.dma_start(offsets[:], offs)
+        nc.sync.dma_start(tracks[:], trk)
+        nc.sync.dma_start(variances[0][:], va_rows[0])
+        for q in range(4):
+            nc.sync.dma_start(
+                all_scales[32 * q : 32 * q + 4, :].bitcast(I32), x_scales[0, 4 * q : 4 * q + 4, :].bitcast(I32)
+            )
+        nc.sync.dma_start(all_words[:], x_words[0].rearrange("p n r -> p (n r)").bitcast(I32))
+        nc.sync.dma_start(states[0][:], st_rows[0])
+        nc.sync.dma_start(variances[1][:], va_rows[1])
+        nc.sync.dma_start(w_raw[:], w1.rearrange("(p j) c -> p j c", j=PACK))
+        nc.sync.dma_start(states[1][:], st_rows[1])
+        nc.sync.dma_start(late_variances[:], va.rearrange("(p t) u -> p t u", t=TILES)[:, 2:4, :])
+        for t in range(2, TILES):
+            nc.sync.dma_start(states[t][:], st_rows[t])
+
+        x_codes = keep.tile([P, S], U32, name="x_codes", align_bytes=64)
+        x_bytes = keep.tile([P, S], U8, name="x_bytes", align_bytes=64)
+        banks = [psum.tile([P, S], F32, name="bank%d" % t) for t in range(TILES)]
+        w_cols = w_raw[:].rearrange("p j (m t) -> p t m j", t=TILES)
+        grouped = [keep.tile([P, P, PACK], BF16, name="grouped%d" % t, align_bytes=64) for t in range(TILES)]
+        dense = [keep.tile([P, U], F32, name="dense%d" % t) for t in range(TILES)]
+        roots = [keep.tile([P, S], F32, name="roots%d" % t) for t in range(2)]
+        keeps = [keep.tile([P, S], F32, name="keeps%d" % t) for t in range(TILES)]
+        gains = [keep.tile([P, S], F32, name="gains%d" % t) for t in range(TILES)]
+        first = [keep.tile([P, S], F32, name="first%d" % t) for t in range(TILES)]
+        second = [keep.tile([P, S], F32, name="second%d" % t) for t in range(TILES)]
+
+        def product(t):
+            w_codes = keep.tile([P, P], U32, name="w_codes%d" % t, align_bytes=64)
+            w_bytes = keep.tile([P, P], U8, name="w_bytes%d" % t, align_bytes=64)
+            nc.vector.quantize_mx(
+                out=w_codes[:].bitcast(FP8X4), scales=w_bytes[:], in_=grouped[t][:].rearrange("p m j -> p (m j)")
+            )
+            nc.tensor.matmul_mx(
+                out=banks[t][:],
+                lhsT=w_codes[:].bitcast(FP8X4),
+                lhsT_scale=w_bytes[:],
+                rhs=x_codes[:].bitcast(FP8X4),
+                rhs_scale=x_bytes[:],
+                start=True,
+                stop=True,
+            )
+
+        def gain(t):
+            nc.scalar.activation(gains[t][:], keeps[t][:], ACT.Copy, bias=1.0, scale=-1.0)
+
+        def root(t):
+            nc.scalar.activation(dense[t][:], variances[t][:], ACT.Abs_reciprocal_sqrt, bias=1.0, scale=2.0)
+            nc.vector.tensor_copy(roots[t][:], dense[t][:].indirect(tracks[:]))
+
+        def square(t):
+            nc.scalar.activation(keeps[t][:], roots[t][:], ACT.Square)
+            gain(t)
+
+        def kept(t):
+            nc.vector.tensor_tensor(first[t][:], states[t][:].indirect(tracks[:]), keeps[t][:], ALU.mult)
+
+        def measured(t):
+            nc.vector.tensor_tensor(second[t][:], gains[t][:], banks[t][:], ALU.mult)
+
+        def scatter(t):
+            nc.vector.tensor_tensor(states[t][:].indirect(tracks[:]), first[t][:], second[t][:], ALU.add)
+            nc.sync.dma_start(out_rows[t], states[t][:])
+
+        nc.vector.tensor_copy(x_bytes[:], all_scales[:].indirect(offsets[:]))
+        root(0)
+        square(0)
+        nc.vector.tensor_copy(x_codes[:], all_words[:].bitcast(U32).indirect(offsets[:]))
+        kept(0)
+        root(1)
+        nc.vector.tensor_copy(grouped[0][:], w_cols[:, 0])
+        product(0)
+        nc.scalar.copy(grouped[1][:], w_cols[:, 1])
+        square(1)
+        for t in range(2, TILES):
+            nc.scalar.activation(dense[t][:], late_variances[:, t - 2, :], ACT.Ln, bias=1.0, scale=2.0)
+        kept(1)
+        product(1)
+        measured(0)
+        scatter(0)
+        for t in range(2, TILES):
+            nc.scalar.activation(keeps[t][:], dense[t][:].indirect(tracks[:]), ACT.Exp, scale=-1.0)
+            nc.scalar.copy(grouped[t][:], w_cols[:, t])
+            gain(t)
+        for t in range(1, TILES):
+            measured(t)
+            if t + 1 < TILES:
+                product(t + 1)
+                kept(t + 1)
+            scatter(t)

@@ -36,9 +36,7 @@ def tile_picked_kalman8_none_p_kernel(tc, x_words, x_scales, w1, st, va, offs, t
         all_words = keep.tile([P, T], I32, name="all_words", align_bytes=64)
         w_raw = keep.tile([P, PACK, N], F32, name="w_raw")
         states = [keep.tile([P, U], F32, name="states%d" % t) for t in range(TILES)]
-
-        variances = [keep.tile([P, U], F32, name="variances%d" % t) for t in range(2)]
-        late_variances = keep.tile([P, 2, U], F32, name="late_variances")
+        variances = [keep.tile([P, U], F32, name="variances%d" % t, tag="variances%d" % t, align_bytes=64) for t in range(TILES)]
 
         nc.vector.memset(all_scales[:].bitcast(I32), 0)
         nc.sync.dma_start(offsets[:], offs)
@@ -48,87 +46,99 @@ def tile_picked_kalman8_none_p_kernel(tc, x_words, x_scales, w1, st, va, offs, t
             nc.sync.dma_start(
                 all_scales[32 * q : 32 * q + 4, :].bitcast(I32), x_scales[0, 4 * q : 4 * q + 4, :].bitcast(I32)
             )
+        nc.sync.dma_start(w_raw[:], w1.rearrange("(p j) c -> p j c", j=PACK))
         nc.sync.dma_start(all_words[:], x_words[0].rearrange("p n r -> p (n r)").bitcast(I32))
         nc.sync.dma_start(states[0][:], st_rows[0])
         nc.sync.dma_start(variances[1][:], va_rows[1])
-        nc.sync.dma_start(w_raw[:], w1.rearrange("(p j) c -> p j c", j=PACK))
+        nc.sync.dma_start(variances[2][:], va_rows[2])
         nc.sync.dma_start(states[1][:], st_rows[1])
-        nc.sync.dma_start(late_variances[:], va.rearrange("(p t) u -> p t u", t=TILES)[:, 2:4, :])
-        for t in range(2, TILES):
-            nc.sync.dma_start(states[t][:], st_rows[t])
+        nc.sync.dma_start(states[2][:], st_rows[2])
+        nc.sync.dma_start(variances[3][:], va_rows[3])
+        nc.sync.dma_start(states[3][:], st_rows[3])
 
         x_codes = keep.tile([P, S], U32, name="x_codes", align_bytes=64)
         x_bytes = keep.tile([P, S], U8, name="x_bytes", align_bytes=64)
         banks = [psum.tile([P, S], F32, name="bank%d" % t) for t in range(TILES)]
         w_cols = w_raw[:].rearrange("p j (m t) -> p t m j", t=TILES)
-        grouped = [keep.tile([P, P, PACK], BF16, name="grouped%d" % t, align_bytes=64) for t in range(TILES)]
-        dense = [keep.tile([P, U], F32, name="dense%d" % t) for t in range(TILES)]
-        roots = [keep.tile([P, S], F32, name="roots%d" % t) for t in range(2)]
+        logs = [keep.tile([P, U], F32, name="logs%d" % t, tag="logs%d" % t, align_bytes=64) for t in range(TILES)]
         keeps = [keep.tile([P, S], F32, name="keeps%d" % t) for t in range(TILES)]
-        gains = [keep.tile([P, S], F32, name="gains%d" % t) for t in range(TILES)]
-        first = [keep.tile([P, S], F32, name="first%d" % t) for t in range(TILES)]
-        second = [keep.tile([P, S], F32, name="second%d" % t) for t in range(TILES)]
+        terms = [keep.tile([P, S], F32, name="terms%d" % t) for t in range(TILES)]
 
-        def product(t):
-            w_codes = keep.tile([P, P], U32, name="w_codes%d" % t, align_bytes=64)
-            w_bytes = keep.tile([P, P], U8, name="w_bytes%d" % t, align_bytes=64)
+        def quantise(grouped, name):
+            width = grouped.shape[1] * P
+            w_codes = keep.tile([P, width], U32, name="w_codes" + name, align_bytes=64)
+            w_bytes = keep.tile([P, width], U8, name="w_bytes" + name, align_bytes=64)
             nc.vector.quantize_mx(
-                out=w_codes[:].bitcast(FP8X4), scales=w_bytes[:], in_=grouped[t][:].rearrange("p m j -> p (m j)")
+                out=w_codes[:].bitcast(FP8X4), scales=w_bytes[:], in_=grouped[:].rearrange("p t m j -> p (t m j)")
             )
+            return [(w_codes[:, c : c + P], w_bytes[:, c : c + P]) for c in range(0, width, P)]
+
+        def product(t, w_codes, w_bytes):
             nc.tensor.matmul_mx(
                 out=banks[t][:],
-                lhsT=w_codes[:].bitcast(FP8X4),
-                lhsT_scale=w_bytes[:],
+                lhsT=w_codes.bitcast(FP8X4),
+                lhsT_scale=w_bytes,
                 rhs=x_codes[:].bitcast(FP8X4),
                 rhs_scale=x_bytes[:],
                 start=True,
                 stop=True,
             )
 
-        def gain(t):
-            nc.scalar.activation(gains[t][:], keeps[t][:], ACT.Copy, bias=1.0, scale=-1.0)
+        def logarithm(t):
+            nc.scalar.activation(logs[t][:], variances[t][:], ACT.Ln, bias=1.0, scale=2.0)
 
-        def root(t):
-            nc.scalar.activation(dense[t][:], variances[t][:], ACT.Abs_reciprocal_sqrt, bias=1.0, scale=2.0)
-            nc.vector.tensor_copy(roots[t][:], dense[t][:].indirect(tracks[:]))
+        def look_up_keep(t):
+            nc.scalar.activation(keeps[t][:], logs[t][:].indirect(tracks[:]), ACT.Exp, scale=-1.0)
 
-        def square(t):
-            nc.scalar.activation(keeps[t][:], roots[t][:], ACT.Square)
-            gain(t)
-
-        def kept(t):
-            nc.vector.tensor_tensor(first[t][:], states[t][:].indirect(tracks[:]), keeps[t][:], ALU.mult)
-
-        def measured(t):
-            nc.vector.tensor_tensor(second[t][:], gains[t][:], banks[t][:], ALU.mult)
-
-        def scatter(t):
-            nc.vector.tensor_tensor(states[t][:].indirect(tracks[:]), first[t][:], second[t][:], ALU.add)
+        def scatter(t, other):
+            nc.vector.tensor_tensor(states[t][:].indirect(tracks[:]), terms[t][:], other[:], ALU.add)
             nc.sync.dma_start(out_rows[t], states[t][:])
 
         nc.vector.tensor_copy(x_bytes[:], all_scales[:].indirect(offsets[:]))
-        root(0)
-        square(0)
+        logarithm(0)
+        look_up_keep(0)
+        gain0 = keep.tile([P, S], F32, name="gain0")
+        nc.scalar.activation(gain0[:], keeps[0][:], ACT.Copy, bias=1.0, scale=-1.0)
+
+        grouped = keep.tile([P, TILES, P, PACK], BF16, name="grouped", align_bytes=64)
+        for t in range(TILES):
+            nc.vector.tensor_copy(grouped[:, t], w_cols[:, t])
+        weights = quantise(grouped, "a")
         nc.vector.tensor_copy(x_codes[:], all_words[:].bitcast(U32).indirect(offsets[:]))
-        kept(0)
-        root(1)
-        nc.vector.tensor_copy(grouped[0][:], w_cols[:, 0])
-        product(0)
-        nc.scalar.copy(grouped[1][:], w_cols[:, 1])
-        square(1)
-        for t in range(2, TILES):
-            nc.scalar.activation(dense[t][:], late_variances[:, t - 2, :], ACT.Ln, bias=1.0, scale=2.0)
-        kept(1)
-        product(1)
-        measured(0)
-        scatter(0)
-        for t in range(2, TILES):
-            nc.scalar.activation(keeps[t][:], dense[t][:].indirect(tracks[:]), ACT.Exp, scale=-1.0)
-            nc.scalar.copy(grouped[t][:], w_cols[:, t])
-            gain(t)
-        for t in range(1, TILES):
-            measured(t)
-            if t + 1 < TILES:
-                product(t + 1)
-                kept(t + 1)
-            scatter(t)
+        nc.vector.tensor_tensor(terms[0][:], states[0][:].indirect(tracks[:]), keeps[0][:], ALU.mult)
+        for t in range(TILES):
+            product(t, *weights[t])
+        nc.vector.tensor_tensor(keeps[0][:], gain0[:], banks[0][:], ALU.mult)
+        scatter(0, keeps[0])
+
+        def measured(t, tag):
+            y = keep.tile([P, S], F32, name="measured%d" % t, tag=tag, align_bytes=64)
+            nc.scalar.copy(y[:], banks[t][:])
+            return y
+
+        diffs = [keep.tile([P, S], F32, name="diffs%d" % t) for t in range(TILES)]
+
+        def differ(t, y):
+            nc.vector.tensor_tensor(diffs[t][:], states[t][:].indirect(tracks[:]), y[:], ALU.subtract)
+
+        def weigh(t):
+            nc.vector.tensor_tensor(terms[t][:], keeps[t][:], diffs[t][:], ALU.mult)
+
+        logarithm(1)
+        y1 = measured(1, "variances1")
+        logarithm(2)
+        look_up_keep(1)
+        y2 = measured(2, "variances2")
+        look_up_keep(2)
+        y3 = measured(3, "logs1")
+        logarithm(3)
+        look_up_keep(3)
+        differ(1, y1)
+        weigh(1)
+        differ(2, y2)
+        scatter(1, y1)
+        weigh(2)
+        differ(3, y3)
+        scatter(2, y2)
+        weigh(3)
+        scatter(3, y3)

@@ -39,9 +39,9 @@ def tile_picked_kalman8_none_p_kernel(tc, x_words, x_scales, w1, st, va, offs, t
         variances = [keep.tile([P, U], F32, name="variances%d" % t, tag="variances%d" % t, align_bytes=64) for t in range(TILES)]
 
         nc.vector.memset(all_scales[:].bitcast(I32), 0)
+        nc.sync.dma_start(variances[0][:], va_rows[0])
         nc.sync.dma_start(offsets[:], offs)
         nc.sync.dma_start(tracks[:], trk)
-        nc.sync.dma_start(variances[0][:], va_rows[0])
         for q in range(4):
             nc.sync.dma_start(
                 all_scales[32 * q : 32 * q + 4, :].bitcast(I32), x_scales[0, 4 * q : 4 * q + 4, :].bitcast(I32)
@@ -59,7 +59,6 @@ def tile_picked_kalman8_none_p_kernel(tc, x_words, x_scales, w1, st, va, offs, t
         x_codes = keep.tile([P, S], U32, name="x_codes", align_bytes=64)
         x_bytes = keep.tile([P, S], U8, name="x_bytes", align_bytes=64)
         banks = [psum.tile([P, S], F32, name="bank%d" % t) for t in range(TILES)]
-        w_cols = w_raw[:].rearrange("p j (m t) -> p t m j", t=TILES)
         logs = [keep.tile([P, U], F32, name="logs%d" % t, tag="logs%d" % t, align_bytes=64) for t in range(TILES)]
         keeps = [keep.tile([P, S], F32, name="keeps%d" % t) for t in range(TILES)]
         terms = [keep.tile([P, S], F32, name="terms%d" % t) for t in range(TILES)]
@@ -101,8 +100,9 @@ def tile_picked_kalman8_none_p_kernel(tc, x_words, x_scales, w1, st, va, offs, t
         nc.scalar.activation(gain0[:], keeps[0][:], ACT.Copy, bias=1.0, scale=-1.0)
 
         grouped = keep.tile([P, TILES, P, PACK], BF16, name="grouped", align_bytes=64)
-        for t in range(TILES):
-            nc.vector.tensor_copy(grouped[:, t], w_cols[:, t])
+        nc.vector.tensor_copy(
+            grouped[:].rearrange("p t m j -> p m t j"), w_raw[:].rearrange("p j (m t) -> p m t j", t=TILES)
+        )
         weights = quantise(grouped, "a")
         nc.vector.tensor_copy(x_codes[:], all_words[:].bitcast(U32).indirect(offsets[:]))
         nc.vector.tensor_tensor(terms[0][:], states[0][:].indirect(tracks[:]), keeps[0][:], ALU.mult)

@@ -90,7 +90,7 @@ def tile_picked_kalman8_none_p_kernel(tc, x_words, x_scales, w1, st, va, offs, t
             nc.scalar.activation(keeps[t][:], logs[t][:].indirect(tracks[:]), ACT.Exp, scale=-1.0)
 
         def scatter(t, other):
-            nc.vector.tensor_tensor(states[t][:].indirect(tracks[:]), terms[t][:], other[:], ALU.add)
+            nc.vector.tensor_tensor(states[t][:].indirect(tracks[:]), terms[t][:], other, ALU.add)
             nc.sync.dma_start(out_rows[t], states[t][:])
 
         nc.vector.tensor_copy(x_bytes[:], all_scales[:].indirect(offsets[:]))
@@ -109,33 +109,34 @@ def tile_picked_kalman8_none_p_kernel(tc, x_words, x_scales, w1, st, va, offs, t
         for t in range(TILES):
             product(t, *weights[t])
         nc.vector.tensor_tensor(keeps[0][:], gain0[:], banks[0][:], ALU.mult)
-        scatter(0, keeps[0])
+        scatter(0, keeps[0][:])
 
-        def measured(t, tag):
-            y = keep.tile([P, S], F32, name="measured%d" % t, tag=tag, align_bytes=64)
-            nc.scalar.copy(y[:], banks[t][:])
+        def measured(t, y):
+            nc.scalar.copy(y, banks[t][:])
             return y
 
         diffs = [keep.tile([P, S], F32, name="diffs%d" % t) for t in range(TILES)]
 
         def differ(t, y):
-            nc.vector.tensor_tensor(diffs[t][:], states[t][:].indirect(tracks[:]), y[:], ALU.subtract)
+            nc.vector.tensor_tensor(diffs[t][:], states[t][:].indirect(tracks[:]), y, ALU.subtract)
 
         def weigh(t):
             nc.vector.tensor_tensor(terms[t][:], keeps[t][:], diffs[t][:], ALU.mult)
 
         logarithm(1)
-        y1 = measured(1, "variances1")
+        early = keep.tile([P, 2 * S], F32, name="early", tag="variances1", align_bytes=64)
+        y1 = measured(1, early[:, :S])
+        y2 = measured(2, early[:, S:])
         logarithm(2)
         look_up_keep(1)
-        y2 = measured(2, "variances2")
         look_up_keep(2)
-        y3 = measured(3, "logs1")
+        late = keep.tile([P, S], F32, name="late", tag="logs1", align_bytes=64)
+        y3 = measured(3, late[:])
         logarithm(3)
         look_up_keep(3)
         differ(1, y1)
-        weigh(1)
         differ(2, y2)
+        weigh(1)
         scatter(1, y1)
         weigh(2)
         differ(3, y3)

@@ -18,76 +18,60 @@ ACT = mybir.ActivationFunctionType
 P = 128
 PACK = 4
 TILES = N // P
+GROUP = 16
+QUADRANT = 32
+SCALE_ROWS = 4
+ALIGN = 64
 
 
 def tile_picked_kalman8_none_p_kernel(tc, x_words, x_scales, w1, st, va, offs, trk, out):
     nc = tc.nc
     with ExitStack() as ctx:
-        keep = ctx.enter_context(tc.tile_pool(name="keep", bufs=1))
+        sbuf = ctx.enter_context(tc.tile_pool(name="keep", bufs=1))
         psum = ctx.enter_context(tc.psum_pool(name="psum", bufs=1))
 
         st_rows = st.rearrange("(p t) u -> t p u", t=TILES)
         va_rows = va.rearrange("(p t) u -> t p u", t=TILES)
         out_rows = out.rearrange("(p t) u -> t p u", t=TILES)
 
-        offsets = keep.tile([P, S // 16], U16, name="offsets")
-        tracks = keep.tile([P, S // 16], U16, name="tracks")
-        all_scales = keep.tile([P, T], U8, name="all_scales", align_bytes=64)
-        all_words = keep.tile([P, T], I32, name="all_words", align_bytes=64)
-        w_raw = keep.tile([P, PACK, N], F32, name="w_raw")
-        states = [keep.tile([P, U], F32, name="states%d" % t) for t in range(TILES)]
-        variances = [keep.tile([P, U], F32, name="variances%d" % t, tag="variances%d" % t, align_bytes=64) for t in range(TILES)]
+        offsets = sbuf.tile([P, S // GROUP], U16, name="offsets")
+        tracks = sbuf.tile([P, S // GROUP], U16, name="tracks")
+        all_scales = sbuf.tile([P, T], U8, name="all_scales", align_bytes=ALIGN)
+        all_words = sbuf.tile([P, T], I32, name="all_words", align_bytes=ALIGN)
+        w_raw = sbuf.tile([P, PACK, N], F32, name="w_raw")
+        states = [sbuf.tile([P, U], F32, name="states%d" % t) for t in range(TILES)]
+        variances = [
+            sbuf.tile([P, U], F32, name="variances%d" % t, tag="variances%d" % t, align_bytes=ALIGN) for t in range(TILES)
+        ]
 
         nc.vector.memset(all_scales[:].bitcast(I32), 0)
+
         nc.sync.dma_start(variances[0][:], va_rows[0])
         nc.sync.dma_start(offsets[:], offs)
         nc.sync.dma_start(tracks[:], trk)
-        for q in range(4):
-            nc.sync.dma_start(
-                all_scales[32 * q : 32 * q + 4, :].bitcast(I32), x_scales[0, 4 * q : 4 * q + 4, :].bitcast(I32)
-            )
+        for row in range(SCALE_ROWS):
+            nc.sync.dma_start(all_scales[row:P:QUADRANT, :].bitcast(I32), x_scales[0, row : SCALE_ROWS * SCALE_ROWS : SCALE_ROWS, :].bitcast(I32))
         nc.sync.dma_start(w_raw[:], w1.rearrange("(p j) c -> p j c", j=PACK))
         nc.sync.dma_start(all_words[:], x_words[0].rearrange("p n r -> p (n r)").bitcast(I32))
         nc.sync.dma_start(states[0][:], st_rows[0])
-        nc.sync.dma_start(variances[1][:], va_rows[1])
-        nc.sync.dma_start(variances[2][:], va_rows[2])
-        nc.sync.dma_start(states[1][:], st_rows[1])
-        nc.sync.dma_start(states[2][:], st_rows[2])
-        nc.sync.dma_start(variances[3][:], va_rows[3])
-        nc.sync.dma_start(states[3][:], st_rows[3])
+        for group in ((1, 2), (3,)):
+            for t in group:
+                nc.sync.dma_start(variances[t][:], va_rows[t])
+            for t in group:
+                nc.sync.dma_start(states[t][:], st_rows[t])
 
-        x_codes = keep.tile([P, S], U32, name="x_codes", align_bytes=64)
-        x_bytes = keep.tile([P, S], U8, name="x_bytes", align_bytes=64)
+        x_codes = sbuf.tile([P, S], U32, name="x_codes", align_bytes=ALIGN)
+        x_bytes = sbuf.tile([P, S], U8, name="x_bytes", align_bytes=ALIGN)
         banks = [psum.tile([P, S], F32, name="bank%d" % t) for t in range(TILES)]
-        logs = [keep.tile([P, U], F32, name="logs%d" % t, tag="logs%d" % t, align_bytes=64) for t in range(TILES)]
-        keeps = [keep.tile([P, S], F32, name="keeps%d" % t) for t in range(TILES)]
-        terms = [keep.tile([P, S], F32, name="terms%d" % t) for t in range(TILES)]
-
-        def quantise(grouped, name):
-            width = grouped.shape[1] * P
-            w_codes = keep.tile([P, width], U32, name="w_codes" + name, align_bytes=64)
-            w_bytes = keep.tile([P, width], U8, name="w_bytes" + name, align_bytes=64)
-            nc.vector.quantize_mx(
-                out=w_codes[:].bitcast(FP8X4), scales=w_bytes[:], in_=grouped[:].rearrange("p t m j -> p (t m j)")
-            )
-            return [(w_codes[:, c : c + P], w_bytes[:, c : c + P]) for c in range(0, width, P)]
-
-        def product(t, w_codes, w_bytes):
-            nc.tensor.matmul_mx(
-                out=banks[t][:],
-                lhsT=w_codes.bitcast(FP8X4),
-                lhsT_scale=w_bytes,
-                rhs=x_codes[:].bitcast(FP8X4),
-                rhs_scale=x_bytes[:],
-                start=True,
-                stop=True,
-            )
+        logs = [sbuf.tile([P, U], F32, name="logs%d" % t, tag="logs%d" % t, align_bytes=ALIGN) for t in range(TILES)]
+        stays = [sbuf.tile([P, S], F32, name="keeps%d" % t) for t in range(TILES)]
+        terms = [sbuf.tile([P, S], F32, name="terms%d" % t) for t in range(TILES)]
 
         def logarithm(t):
             nc.scalar.activation(logs[t][:], variances[t][:], ACT.Ln, bias=1.0, scale=2.0)
 
-        def look_up_keep(t):
-            nc.scalar.activation(keeps[t][:], logs[t][:].indirect(tracks[:]), ACT.Exp, scale=-1.0)
+        def look_up_stay(t):
+            nc.scalar.activation(stays[t][:], logs[t][:].indirect(tracks[:]), ACT.Exp, scale=-1.0)
 
         def scatter(t, other):
             nc.vector.tensor_tensor(states[t][:].indirect(tracks[:]), terms[t][:], other, ALU.add)
@@ -95,45 +79,58 @@ def tile_picked_kalman8_none_p_kernel(tc, x_words, x_scales, w1, st, va, offs, t
 
         nc.vector.tensor_copy(x_bytes[:], all_scales[:].indirect(offsets[:]))
         logarithm(0)
-        look_up_keep(0)
-        gain0 = keep.tile([P, S], F32, name="gain0")
-        nc.scalar.activation(gain0[:], keeps[0][:], ACT.Copy, bias=1.0, scale=-1.0)
+        look_up_stay(0)
+        gain0 = sbuf.tile([P, S], F32, name="gain0")
+        nc.scalar.activation(gain0[:], stays[0][:], ACT.Copy, bias=1.0, scale=-1.0)
 
-        grouped = keep.tile([P, TILES, P, PACK], BF16, name="grouped", align_bytes=64)
+        grouped = sbuf.tile([P, TILES, P, PACK], BF16, name="grouped", align_bytes=ALIGN)
         nc.vector.tensor_copy(
             grouped[:].rearrange("p t m j -> p m t j"), w_raw[:].rearrange("p j (m t) -> p m t j", t=TILES)
         )
-        weights = quantise(grouped, "a")
+        w_codes = sbuf.tile([P, N], U32, name="w_codesa", align_bytes=ALIGN)
+        w_bytes = sbuf.tile([P, N], U8, name="w_bytesa", align_bytes=ALIGN)
+        nc.vector.quantize_mx(
+            out=w_codes[:].bitcast(FP8X4), scales=w_bytes[:], in_=grouped[:].rearrange("p t m j -> p (t m j)")
+        )
         nc.vector.tensor_copy(x_codes[:], all_words[:].bitcast(U32).indirect(offsets[:]))
-        nc.vector.tensor_tensor(terms[0][:], states[0][:].indirect(tracks[:]), keeps[0][:], ALU.mult)
+
+        nc.vector.tensor_tensor(terms[0][:], states[0][:].indirect(tracks[:]), stays[0][:], ALU.mult)
         for t in range(TILES):
-            product(t, *weights[t])
-        nc.vector.tensor_tensor(keeps[0][:], gain0[:], banks[0][:], ALU.mult)
-        scatter(0, keeps[0][:])
+            cols = slice(P * t, P * (t + 1))
+            nc.tensor.matmul_mx(
+                out=banks[t][:],
+                lhsT=w_codes[:, cols].bitcast(FP8X4),
+                lhsT_scale=w_bytes[:, cols],
+                rhs=x_codes[:].bitcast(FP8X4),
+                rhs_scale=x_bytes[:],
+                start=True,
+                stop=True,
+            )
+        gained0 = stays[0][:]
+        nc.vector.tensor_tensor(gained0, gain0[:], banks[0][:], ALU.mult)
+        scatter(0, gained0)
 
-        def measured(t, y):
-            nc.scalar.copy(y, banks[t][:])
-            return y
-
-        diffs = [keep.tile([P, S], F32, name="diffs%d" % t) for t in range(TILES)]
+        diffs = [sbuf.tile([P, S], F32, name="diffs%d" % t) for t in range(TILES)]
 
         def differ(t, y):
             nc.vector.tensor_tensor(diffs[t][:], states[t][:].indirect(tracks[:]), y, ALU.subtract)
 
         def weigh(t):
-            nc.vector.tensor_tensor(terms[t][:], keeps[t][:], diffs[t][:], ALU.mult)
+            nc.vector.tensor_tensor(terms[t][:], stays[t][:], diffs[t][:], ALU.mult)
 
         logarithm(1)
-        early = keep.tile([P, 2 * S], F32, name="early", tag="variances1", align_bytes=64)
-        y1 = measured(1, early[:, :S])
-        y2 = measured(2, early[:, S:])
+        y12 = sbuf.tile([P, 2 * S], F32, name="early", tag="variances1", align_bytes=ALIGN)
+        y1, y2 = y12[:, :S], y12[:, S:]
+        nc.scalar.copy(y1, banks[1][:])
+        nc.scalar.copy(y2, banks[2][:])
         logarithm(2)
-        look_up_keep(1)
-        look_up_keep(2)
-        late = keep.tile([P, S], F32, name="late", tag="logs1", align_bytes=64)
-        y3 = measured(3, late[:])
+        look_up_stay(1)
+        look_up_stay(2)
+        y3 = sbuf.tile([P, S], F32, name="late", tag="logs1", align_bytes=ALIGN)[:]
+        nc.scalar.copy(y3, banks[3][:])
         logarithm(3)
-        look_up_keep(3)
+        look_up_stay(3)
+
         differ(1, y1)
         differ(2, y2)
         weigh(1)

@@ -54,47 +54,60 @@ def tile_picked_kalman8_none_p_kernel(tc, x_words, x_scales, w1, st, va, offs, t
         nc.sync.dma_start(w_raw[:], w1.rearrange("(p j) c -> p j c", j=PACK))
         nc.sync.dma_start(all_words[:], x_words[0].rearrange("p n r -> p (n r)").bitcast(I32))
         nc.sync.dma_start(states[0][:], st_rows[0])
-        for group in ((1, 2), (3,)):
-            for t in group:
-                nc.sync.dma_start(variances[t][:], va_rows[t])
-            for t in group:
-                nc.sync.dma_start(states[t][:], st_rows[t])
+        for t in (1, 2):
+            nc.sync.dma_start(variances[t][:], va_rows[t])
+        for t in (1, 2, 3):
+            nc.sync.dma_start(states[t][:], st_rows[t])
+        nc.sync.dma_start(variances[3][:], va_rows[3])
 
         x_codes = sbuf.tile([P, S], U32, name="x_codes", align_bytes=ALIGN)
         x_bytes = sbuf.tile([P, S], U8, name="x_bytes", align_bytes=ALIGN)
         banks = [psum.tile([P, S], F32, name="bank%d" % t) for t in range(TILES)]
         logs = [sbuf.tile([P, U], F32, name="logs%d" % t, tag="logs%d" % t, align_bytes=ALIGN) for t in range(TILES)]
         stays = [sbuf.tile([P, S], F32, name="keeps%d" % t) for t in range(TILES)]
-        terms = [sbuf.tile([P, S], F32, name="terms%d" % t) for t in range(TILES)]
+
+        whole, first, second = slice(0, S), slice(0, S // 2), slice(S // 2, S)
+
+        def entries(part):
+            return tracks[:, part.start // GROUP : part.stop // GROUP]
 
         def logarithm(t):
             nc.scalar.activation(logs[t][:], variances[t][:], ACT.Ln, bias=1.0, scale=2.0)
 
-        def look_up_stay(t):
-            nc.scalar.activation(stays[t][:], logs[t][:].indirect(tracks[:]), ACT.Exp, scale=-1.0)
+        def look_up_stay(t, part):
+            nc.scalar.activation(stays[t][:, part], logs[t][:].indirect(entries(part)), ACT.Exp, scale=-1.0)
 
-        def scatter(t, other):
-            nc.vector.tensor_tensor(states[t][:].indirect(tracks[:]), terms[t][:], other, ALU.add)
+        def scatter(t, part, term, other):
+            nc.vector.tensor_tensor(states[t][:].indirect(entries(part)), term, other, ALU.add)
+
+        def store(t):
             nc.sync.dma_start(out_rows[t], states[t][:])
 
         nc.vector.tensor_copy(x_bytes[:], all_scales[:].indirect(offsets[:]))
         logarithm(0)
-        look_up_stay(0)
+        look_up_stay(0, whole)
         gain0 = sbuf.tile([P, S], F32, name="gain0")
         nc.scalar.activation(gain0[:], stays[0][:], ACT.Copy, bias=1.0, scale=-1.0)
 
-        grouped = sbuf.tile([P, TILES, P, PACK], BF16, name="grouped", align_bytes=ALIGN)
-        nc.vector.tensor_copy(
-            grouped[:].rearrange("p t m j -> p m t j"), w_raw[:].rearrange("p j (m t) -> p m t j", t=TILES)
-        )
-        w_codes = sbuf.tile([P, N], U32, name="w_codesa", align_bytes=ALIGN)
-        w_bytes = sbuf.tile([P, N], U8, name="w_bytesa", align_bytes=ALIGN)
-        nc.vector.quantize_mx(
-            out=w_codes[:].bitcast(FP8X4), scales=w_bytes[:], in_=grouped[:].rearrange("p t m j -> p (t m j)")
-        )
+        pairs = (slice(0, 2), slice(2, 4))
+        grouped = [sbuf.tile([P, 2, P, PACK], BF16, name="grouped%d" % h, align_bytes=ALIGN) for h in range(2)]
+        for h in range(2):
+            nc.vector.tensor_copy(
+                grouped[h][:].rearrange("p t m j -> p m t j"),
+                w_raw[:].rearrange("p j (m t) -> p m t j", t=TILES)[:, :, pairs[h], :],
+            )
+        w_codes = sbuf.tile([P, N], U32, name="w_codes", align_bytes=ALIGN)
+        w_bytes = sbuf.tile([P, N], U8, name="w_bytes", align_bytes=ALIGN)
+        for h in range(2):
+            cols = slice(2 * P * h, 2 * P * (h + 1))
+            nc.vector.quantize_mx(
+                out=w_codes[:, cols].bitcast(FP8X4), scales=w_bytes[:, cols], in_=grouped[h][:].rearrange("p t m j -> p (t m j)")
+            )
         nc.vector.tensor_copy(x_codes[:], all_words[:].bitcast(U32).indirect(offsets[:]))
 
-        nc.vector.tensor_tensor(terms[0][:], states[0][:].indirect(tracks[:]), stays[0][:], ALU.mult)
+        kept0 = sbuf.tile([P, S], F32, name="kept0")
+        for part in (first, second):
+            nc.vector.tensor_tensor(kept0[:, part], states[0][:].indirect(entries(part)), stays[0][:, part], ALU.mult)
         for t in range(TILES):
             cols = slice(P * t, P * (t + 1))
             nc.tensor.matmul_mx(
@@ -106,17 +119,18 @@ def tile_picked_kalman8_none_p_kernel(tc, x_words, x_scales, w1, st, va, offs, t
                 start=True,
                 stop=True,
             )
-        gained0 = stays[0][:]
-        nc.vector.tensor_tensor(gained0, gain0[:], banks[0][:], ALU.mult)
-        scatter(0, gained0)
+        for part in (first, second):
+            nc.vector.tensor_tensor(stays[0][:, part], gain0[:, part], banks[0][:, part], ALU.mult)
+        scatter(0, whole, kept0[:], stays[0][:])
+        store(0)
 
         diffs = [sbuf.tile([P, S], F32, name="diffs%d" % t) for t in range(TILES)]
 
         def differ(t, y):
             nc.vector.tensor_tensor(diffs[t][:], states[t][:].indirect(tracks[:]), y, ALU.subtract)
 
-        def weigh(t):
-            nc.vector.tensor_tensor(terms[t][:], stays[t][:], diffs[t][:], ALU.mult)
+        def weigh(t, part, term):
+            nc.vector.tensor_tensor(term, stays[t][:, part], diffs[t][:, part], ALU.mult)
 
         logarithm(1)
         y12 = sbuf.tile([P, 2 * S], F32, name="early", tag="variances1", align_bytes=ALIGN)
@@ -124,19 +138,29 @@ def tile_picked_kalman8_none_p_kernel(tc, x_words, x_scales, w1, st, va, offs, t
         nc.scalar.copy(y1, banks[1][:])
         nc.scalar.copy(y2, banks[2][:])
         logarithm(2)
-        look_up_stay(1)
-        look_up_stay(2)
-        y3 = sbuf.tile([P, S], F32, name="late", tag="logs1", align_bytes=ALIGN)[:]
+        y3 = sbuf.tile([P, S], F32, name="late", tag="variances2", align_bytes=ALIGN)[:]
         nc.scalar.copy(y3, banks[3][:])
+        look_up_stay(1, whole)
+        look_up_stay(2, first)
+        look_up_stay(2, second)
         logarithm(3)
-        look_up_stay(3)
+        look_up_stay(3, whole)
 
         differ(1, y1)
         differ(2, y2)
-        weigh(1)
-        scatter(1, y1)
-        weigh(2)
         differ(3, y3)
-        scatter(2, y2)
-        weigh(3)
-        scatter(3, y3)
+        term1 = sbuf.tile([P, S], F32, name="term1")[:]
+        term2a = sbuf.tile([P, S // 2], F32, name="term2a")[:]
+        term2b = sbuf.tile([P, S // 2], F32, name="term2b", tag="logs3", align_bytes=ALIGN)[:]
+        term3 = sbuf.tile([P, S], F32, name="term3")[:]
+        weigh(1, whole, term1)
+        weigh(2, first, term2a)
+        scatter(1, whole, term1, y1)
+        store(1)
+        scatter(2, first, term2a, y2[:, first])
+        weigh(2, second, term2b)
+        weigh(3, whole, term3)
+        scatter(2, second, term2b, y2[:, second])
+        store(2)
+        scatter(3, whole, term3, y3)
+        store(3)

@@ -21,6 +21,7 @@ TILES = N // P
 GROUP = 16
 QUADRANT = 32
 SCALE_ROWS = 4
+SPREAD = QUADRANT // SCALE_ROWS
 ALIGN = 64
 
 
@@ -49,10 +50,15 @@ def tile_picked_kalman8_none_p_kernel(tc, x_words, x_scales, w1, st, va, offs, t
         nc.sync.dma_start(variances[0][:], va_rows[0])
         nc.sync.dma_start(offsets[:], offs)
         nc.sync.dma_start(tracks[:], trk)
-        for row in range(SCALE_ROWS):
-            nc.sync.dma_start(all_scales[row:P:QUADRANT, :].bitcast(I32), x_scales[0, row : SCALE_ROWS * SCALE_ROWS : SCALE_ROWS, :].bitcast(I32))
+        nc.sync.dma_start(all_scales[0:P:SPREAD, :].bitcast(I32), x_scales[0].bitcast(I32))
         nc.sync.dma_start(w_raw[:], w1.rearrange("(p j) c -> p j c", j=PACK))
         nc.sync.dma_start(all_words[:], x_words[0].rearrange("p n r -> p (n r)").bitcast(I32))
+        picked_bytes = sbuf.tile([P, S], U8, name="picked_bytes", align_bytes=ALIGN)
+        x_bytes = sbuf.tile([P, S], U8, name="x_bytes", align_bytes=ALIGN)
+        nc.vector.memset(x_bytes[:].bitcast(I32), 0)
+        nc.vector.tensor_copy(picked_bytes[:], all_scales[:].indirect(offsets[:]))
+        for row in range(SCALE_ROWS):
+            nc.sync.dma_start(x_bytes[row:P:QUADRANT, :].bitcast(I32), picked_bytes[SPREAD * row : P : QUADRANT, :].bitcast(I32))
         nc.sync.dma_start(states[0][:], st_rows[0])
         for t in (1, 2):
             nc.sync.dma_start(variances[t][:], va_rows[t])
@@ -61,7 +67,6 @@ def tile_picked_kalman8_none_p_kernel(tc, x_words, x_scales, w1, st, va, offs, t
         nc.sync.dma_start(variances[3][:], va_rows[3])
 
         x_codes = sbuf.tile([P, S], U32, name="x_codes", align_bytes=ALIGN)
-        x_bytes = sbuf.tile([P, S], U8, name="x_bytes", align_bytes=ALIGN)
         banks = [psum.tile([P, S], F32, name="bank%d" % t) for t in range(TILES)]
         logs = [sbuf.tile([P, U], F32, name="logs%d" % t, tag="logs%d" % t, align_bytes=ALIGN) for t in range(TILES)]
         stays = [sbuf.tile([P, S], F32, name="keeps%d" % t) for t in range(TILES)]
@@ -74,8 +79,8 @@ def tile_picked_kalman8_none_p_kernel(tc, x_words, x_scales, w1, st, va, offs, t
         def logarithm(t):
             nc.scalar.activation(logs[t][:], variances[t][:], ACT.Ln, bias=1.0, scale=2.0)
 
-        def look_up_stay(t, part):
-            nc.scalar.activation(stays[t][:, part], logs[t][:].indirect(entries(part)), ACT.Exp, scale=-1.0)
+        def look_up_stay(t, part, stay):
+            nc.scalar.activation(stay, logs[t][:].indirect(entries(part)), ACT.Exp, scale=-1.0)
 
         def scatter(t, part, term, other):
             nc.vector.tensor_tensor(states[t][:].indirect(entries(part)), term, other, ALU.add)
@@ -83,9 +88,8 @@ def tile_picked_kalman8_none_p_kernel(tc, x_words, x_scales, w1, st, va, offs, t
         def store(t):
             nc.sync.dma_start(out_rows[t], states[t][:])
 
-        nc.vector.tensor_copy(x_bytes[:], all_scales[:].indirect(offsets[:]))
         logarithm(0)
-        look_up_stay(0, whole)
+        look_up_stay(0, whole, stays[0][:])
         gain0 = sbuf.tile([P, S], F32, name="gain0")
         nc.scalar.activation(gain0[:], stays[0][:], ACT.Copy, bias=1.0, scale=-1.0)
 
@@ -129,8 +133,8 @@ def tile_picked_kalman8_none_p_kernel(tc, x_words, x_scales, w1, st, va, offs, t
         def differ(t, y):
             nc.vector.tensor_tensor(diffs[t][:], states[t][:].indirect(tracks[:]), y, ALU.subtract)
 
-        def weigh(t, part, term):
-            nc.vector.tensor_tensor(term, stays[t][:, part], diffs[t][:, part], ALU.mult)
+        def weigh(t, part, stay, term):
+            nc.vector.tensor_tensor(term, stay, diffs[t][:, part], ALU.mult)
 
         logarithm(1)
         y12 = sbuf.tile([P, 2 * S], F32, name="early", tag="variances1", align_bytes=ALIGN)
@@ -140,27 +144,27 @@ def tile_picked_kalman8_none_p_kernel(tc, x_words, x_scales, w1, st, va, offs, t
         logarithm(2)
         y3 = sbuf.tile([P, S], F32, name="late", tag="variances2", align_bytes=ALIGN)[:]
         nc.scalar.copy(y3, banks[3][:])
-        look_up_stay(1, whole)
-        look_up_stay(2, first)
-        look_up_stay(2, second)
+        look_up_stay(1, whole, stays[1][:])
+        look_up_stay(2, first, stays[2][:, first])
         logarithm(3)
-        look_up_stay(3, whole)
+        look_up_stay(3, first, stays[3][:, first])
+        look_up_stay(3, second, stays[3][:, second])
+        stay2b = sbuf.tile([P, S // 2], F32, name="stay2b", tag="variances3", align_bytes=ALIGN)[:]
+        look_up_stay(2, second, stay2b)
 
         differ(1, y1)
         differ(2, y2)
         differ(3, y3)
-        term1 = sbuf.tile([P, S], F32, name="term1")[:]
-        term2a = sbuf.tile([P, S // 2], F32, name="term2a")[:]
-        term2b = sbuf.tile([P, S // 2], F32, name="term2b", tag="logs3", align_bytes=ALIGN)[:]
-        term3 = sbuf.tile([P, S], F32, name="term3")[:]
-        weigh(1, whole, term1)
-        weigh(2, first, term2a)
-        scatter(1, whole, term1, y1)
+        terms = [sbuf.tile([P, S], F32, name="terms%d" % t) for t in range(TILES)]
+        weigh(1, whole, stays[1][:], terms[1][:])
+        weigh(2, first, stays[2][:, first], terms[2][:, first])
+        scatter(1, whole, terms[1][:], y1)
         store(1)
-        scatter(2, first, term2a, y2[:, first])
-        weigh(2, second, term2b)
-        weigh(3, whole, term3)
-        scatter(2, second, term2b, y2[:, second])
-        store(2)
-        scatter(3, whole, term3, y3)
+        scatter(2, first, terms[2][:, first], y2[:, first])
+        weigh(3, first, stays[3][:, first], terms[3][:, first])
+        weigh(3, second, stays[3][:, second], terms[3][:, second])
+        weigh(2, second, stay2b, terms[2][:, second])
+        scatter(3, whole, terms[3][:], y3)
         store(3)
+        scatter(2, second, terms[2][:, second], y2[:, second])
+        store(2)

@@ -53,13 +53,13 @@ def tile_picked_kalman8_none_p_kernel(tc, x_words, x_scales, w1, st, va, offs, t
         nc.sync.dma_start(all_scales[0:P:SPREAD, :].bitcast(I32), x_scales[0].bitcast(I32))
         nc.sync.dma_start(w_raw[:], w1.rearrange("(p j) c -> p j c", j=PACK))
         nc.sync.dma_start(all_words[:], x_words[0].rearrange("p n r -> p (n r)").bitcast(I32))
+        nc.sync.dma_start(states[0][:], st_rows[0])
         picked_bytes = sbuf.tile([P, S], U8, name="picked_bytes", align_bytes=ALIGN)
         x_bytes = sbuf.tile([P, S], U8, name="x_bytes", align_bytes=ALIGN)
         nc.vector.memset(x_bytes[:].bitcast(I32), 0)
         nc.vector.tensor_copy(picked_bytes[:], all_scales[:].indirect(offsets[:]))
         for row in range(SCALE_ROWS):
             nc.sync.dma_start(x_bytes[row:P:QUADRANT, :].bitcast(I32), picked_bytes[SPREAD * row : P : QUADRANT, :].bitcast(I32))
-        nc.sync.dma_start(states[0][:], st_rows[0])
         for t in (1, 2):
             nc.sync.dma_start(variances[t][:], va_rows[t])
         for t in (1, 2, 3):
@@ -90,15 +90,14 @@ def tile_picked_kalman8_none_p_kernel(tc, x_words, x_scales, w1, st, va, offs, t
 
         logarithm(0)
         look_up_stay(0, whole, stays[0][:])
-        gain0 = sbuf.tile([P, S], F32, name="gain0")
-        nc.scalar.activation(gain0[:], stays[0][:], ACT.Copy, bias=1.0, scale=-1.0)
 
         pairs = (slice(0, 2), slice(2, 4))
         grouped = [sbuf.tile([P, 2, P, PACK], BF16, name="grouped%d" % h, align_bytes=ALIGN) for h in range(2)]
         for h in range(2):
-            nc.vector.tensor_copy(
+            nc.vector.tensor_scalar_mul(
                 grouped[h][:].rearrange("p t m j -> p m t j"),
                 w_raw[:].rearrange("p j (m t) -> p m t j", t=TILES)[:, :, pairs[h], :],
+                -1.0,
             )
         w_codes = sbuf.tile([P, N], U32, name="w_codes", align_bytes=ALIGN)
         w_bytes = sbuf.tile([P, N], U8, name="w_bytes", align_bytes=ALIGN)
@@ -124,7 +123,7 @@ def tile_picked_kalman8_none_p_kernel(tc, x_words, x_scales, w1, st, va, offs, t
                 stop=True,
             )
         for part in (first, second):
-            nc.vector.tensor_tensor(stays[0][:, part], gain0[:, part], banks[0][:, part], ALU.mult)
+            nc.vector.scalar_tensor_tensor(stays[0][:, part], stays[0][:, part], -1.0, banks[0][:, part], ALU.add, ALU.mult)
         scatter(0, whole, kept0[:], stays[0][:])
         store(0)
 
@@ -139,18 +138,18 @@ def tile_picked_kalman8_none_p_kernel(tc, x_words, x_scales, w1, st, va, offs, t
         logarithm(1)
         y12 = sbuf.tile([P, 2 * S], F32, name="early", tag="variances1", align_bytes=ALIGN)
         y1, y2 = y12[:, :S], y12[:, S:]
-        nc.scalar.copy(y1, banks[1][:])
-        nc.scalar.copy(y2, banks[2][:])
+        nc.scalar.activation(y1, banks[1][:], ACT.Copy, scale=-1.0)
+        nc.scalar.activation(y2, banks[2][:], ACT.Copy, scale=-1.0)
         logarithm(2)
         y3 = sbuf.tile([P, S], F32, name="late", tag="variances2", align_bytes=ALIGN)[:]
-        nc.scalar.copy(y3, banks[3][:])
+        nc.scalar.activation(y3, banks[3][:], ACT.Copy, scale=-1.0)
         look_up_stay(1, whole, stays[1][:])
         look_up_stay(2, first, stays[2][:, first])
         logarithm(3)
         look_up_stay(3, first, stays[3][:, first])
-        look_up_stay(3, second, stays[3][:, second])
         stay2b = sbuf.tile([P, S // 2], F32, name="stay2b", tag="variances3", align_bytes=ALIGN)[:]
         look_up_stay(2, second, stay2b)
+        look_up_stay(3, second, stays[3][:, second])
 
         differ(1, y1)
         differ(2, y2)
@@ -162,9 +161,10 @@ def tile_picked_kalman8_none_p_kernel(tc, x_words, x_scales, w1, st, va, offs, t
         store(1)
         scatter(2, first, terms[2][:, first], y2[:, first])
         weigh(3, first, stays[3][:, first], terms[3][:, first])
-        weigh(3, second, stays[3][:, second], terms[3][:, second])
         weigh(2, second, stay2b, terms[2][:, second])
-        scatter(3, whole, terms[3][:], y3)
-        store(3)
+        scatter(3, first, terms[3][:, first], y3[:, first])
+        weigh(3, second, stays[3][:, second], terms[3][:, second])
         scatter(2, second, terms[2][:, second], y2[:, second])
         store(2)
+        scatter(3, second, terms[3][:, second], y3[:, second])
+        store(3)

@@ -144,27 +144,30 @@ def tile_picked_kalman8_none_p_kernel(tc, x_words, x_scales, w1, st, va, offs, t
         y3 = sbuf.tile([P, S], F32, name="late", tag="variances2", align_bytes=ALIGN)[:]
         nc.scalar.activation(y3, banks[3][:], ACT.Copy, scale=-1.0)
         look_up_stay(1, whole, stays[1][:])
-        look_up_stay(2, first, stays[2][:, first])
+        look_up_stay(2, whole, stays[2][:])
         logarithm(3)
-        look_up_stay(3, first, stays[3][:, first])
-        stay2b = sbuf.tile([P, S // 2], F32, name="stay2b", tag="variances3", align_bytes=ALIGN)[:]
-        look_up_stay(2, second, stay2b)
-        look_up_stay(3, second, stays[3][:, second])
+        for part in (first, second):
+            look_up_stay(3, part, stays[3][:, part])
 
         differ(1, y1)
         differ(2, y2)
-        differ(3, y3)
-        terms = [sbuf.tile([P, S], F32, name="terms%d" % t) for t in range(TILES)]
-        weigh(1, whole, stays[1][:], terms[1][:])
-        weigh(2, first, stays[2][:, first], terms[2][:, first])
-        scatter(1, whole, terms[1][:], y1)
-        store(1)
-        scatter(2, first, terms[2][:, first], y2[:, first])
-        weigh(3, first, stays[3][:, first], terms[3][:, first])
-        weigh(2, second, stay2b, terms[2][:, second])
-        scatter(3, first, terms[3][:, first], y3[:, first])
-        weigh(3, second, stays[3][:, second], terms[3][:, second])
-        scatter(2, second, terms[2][:, second], y2[:, second])
-        store(2)
-        scatter(3, second, terms[3][:, second], y3[:, second])
+        terms = sbuf.tile([P, S], F32, name="terms")
+        news = [sbuf.tile([P, S], F32, name="news%d" % t) for t in range(TILES)]
+        for part in (first, second):
+            weigh(1, part, stays[1][:, part], terms[:, part])
+        for part in (first, second):
+            nc.vector.tensor_tensor(news[1][:, part], terms[:, part], y1[:, part], ALU.add)
+        old3 = stays[1]
+        nc.vector.tensor_copy(old3[:], states[3][:].indirect(tracks[:]))
+        nc.gpsimd.tensor_tensor(terms[:], stays[2][:], diffs[2][:], ALU.mult)
+        nc.gpsimd.tensor_tensor(news[2][:], terms[:], y2, ALU.add)
+        nc.gpsimd.tensor_tensor(diffs[3][:], old3[:], y3, ALU.subtract)
+        for part in (first, second):
+            nc.gpsimd.tensor_tensor(terms[:, part], stays[3][:, part], diffs[3][:, part], ALU.mult)
+            nc.gpsimd.tensor_tensor(news[3][:, part], terms[:, part], y3[:, part], ALU.add)
+        for t in (1, 2):
+            nc.vector.tensor_copy(states[t][:].indirect(tracks[:]), news[t][:])
+            store(t)
+        for part in (first, second):
+            nc.vector.tensor_copy(states[3][:].indirect(entries(part)), news[3][:, part])
         store(3)

@@ -141,10 +141,10 @@ def tile_picked_kalman8_none_p_kernel(tc, x_words, x_scales, w1, st, va, offs, t
         nc.scalar.activation(y1, banks[1][:], ACT.Copy, scale=-1.0)
         nc.scalar.activation(y2, banks[2][:], ACT.Copy, scale=-1.0)
         logarithm(2)
-        y3 = sbuf.tile([P, S], F32, name="late", tag="variances2", align_bytes=ALIGN)[:]
-        nc.scalar.activation(y3, banks[3][:], ACT.Copy, scale=-1.0)
         look_up_stay(1, whole, stays[1][:])
         look_up_stay(2, whole, stays[2][:])
+        y3 = sbuf.tile([P, S], F32, name="late", tag="variances2", align_bytes=ALIGN)[:]
+        nc.scalar.activation(y3, banks[3][:], ACT.Copy, scale=-1.0)
         logarithm(3)
         for part in (first, second):
             look_up_stay(3, part, stays[3][:, part])
@@ -153,21 +153,21 @@ def tile_picked_kalman8_none_p_kernel(tc, x_words, x_scales, w1, st, va, offs, t
         differ(2, y2)
         terms = sbuf.tile([P, S], F32, name="terms")
         news = [sbuf.tile([P, S], F32, name="news%d" % t) for t in range(TILES)]
-        for part in (first, second):
-            weigh(1, part, stays[1][:, part], terms[:, part])
-        for part in (first, second):
-            nc.vector.tensor_tensor(news[1][:, part], terms[:, part], y1[:, part], ALU.add)
-        old3 = stays[1]
-        nc.vector.tensor_copy(old3[:], states[3][:].indirect(tracks[:]))
+        old3a = sbuf.tile([P, S // 2], F32, name="old3a", tag="logs1", align_bytes=ALIGN)[:]
+        old3b = stays[1][:, first]
+        weigh(1, whole, stays[1][:], terms[:])
+        nc.vector.tensor_copy(old3a, states[3][:].indirect(entries(first)))
+        nc.vector.tensor_tensor(news[1][:], terms[:], y1, ALU.add)
+        nc.vector.tensor_copy(old3b, states[3][:].indirect(entries(second)))
         nc.gpsimd.tensor_tensor(terms[:], stays[2][:], diffs[2][:], ALU.mult)
         nc.gpsimd.tensor_tensor(news[2][:], terms[:], y2, ALU.add)
-        nc.gpsimd.tensor_tensor(diffs[3][:], old3[:], y3, ALU.subtract)
+        diff3 = y2
+        for part, old in ((first, old3a), (second, old3b)):
+            nc.gpsimd.tensor_tensor(diff3[:, part], old, y3[:, part], ALU.subtract)
         for part in (first, second):
-            nc.gpsimd.tensor_tensor(terms[:, part], stays[3][:, part], diffs[3][:, part], ALU.mult)
-            nc.gpsimd.tensor_tensor(news[3][:, part], terms[:, part], y3[:, part], ALU.add)
+            nc.gpsimd.tensor_tensor(terms[:, part], stays[3][:, part], diff3[:, part], ALU.mult)
         for t in (1, 2):
             nc.vector.tensor_copy(states[t][:].indirect(tracks[:]), news[t][:])
             store(t)
-        for part in (first, second):
-            nc.vector.tensor_copy(states[3][:].indirect(entries(part)), news[3][:, part])
+        scatter(3, whole, terms[:], y3)
         store(3)

@@ -22,6 +22,7 @@ GROUP = 16
 QUADRANT = 32
 SCALE_ROWS = 4
 SPREAD = QUADRANT // SCALE_ROWS
+SHARE = 384
 ALIGN = 64
 
 
@@ -62,7 +63,7 @@ def tile_picked_kalman8_none_p_kernel(tc, x_words, x_scales, w1, st, va, offs, t
             nc.sync.dma_start(x_bytes[row:P:QUADRANT, :].bitcast(I32), picked_bytes[SPREAD * row : P : QUADRANT, :].bitcast(I32))
         for t in (1, 2):
             nc.sync.dma_start(variances[t][:], va_rows[t])
-        for t in (1, 2, 3):
+        for t in (3, 1, 2):
             nc.sync.dma_start(states[t][:], st_rows[t])
         nc.sync.dma_start(variances[3][:], va_rows[3])
 
@@ -127,47 +128,41 @@ def tile_picked_kalman8_none_p_kernel(tc, x_words, x_scales, w1, st, va, offs, t
         scatter(0, whole, kept0[:], stays[0][:])
         store(0)
 
-        diffs = [sbuf.tile([P, S], F32, name="diffs%d" % t) for t in range(TILES)]
-
-        def differ(t, y):
-            nc.vector.tensor_tensor(diffs[t][:], states[t][:].indirect(tracks[:]), y, ALU.subtract)
-
-        def weigh(t, part, stay, term):
-            nc.vector.tensor_tensor(term, stay, diffs[t][:, part], ALU.mult)
-
+        halves = (first, second)
         logarithm(1)
-        y12 = sbuf.tile([P, 2 * S], F32, name="early", tag="variances1", align_bytes=ALIGN)
-        y1, y2 = y12[:, :S], y12[:, S:]
+        y1_old3 = sbuf.tile([P, S + S // 2], F32, name="y1_old3", tag="variances1", align_bytes=ALIGN)
+        old3, y1 = y1_old3[:, :S], y1_old3[:, S // 2 :]
         nc.scalar.activation(y1, banks[1][:], ACT.Copy, scale=-1.0)
-        nc.scalar.activation(y2, banks[2][:], ACT.Copy, scale=-1.0)
         logarithm(2)
         look_up_stay(1, whole, stays[1][:])
         look_up_stay(2, whole, stays[2][:])
-        y3 = sbuf.tile([P, S], F32, name="late", tag="variances2", align_bytes=ALIGN)[:]
+        y2 = sbuf.tile([P, S], F32, name="y2", tag="logs1", align_bytes=ALIGN)[:]
+        nc.scalar.activation(y2, banks[2][:], ACT.Copy, scale=-1.0)
+        y3 = sbuf.tile([P, S], F32, name="y3", tag="variances2", align_bytes=ALIGN)[:]
         nc.scalar.activation(y3, banks[3][:], ACT.Copy, scale=-1.0)
         logarithm(3)
-        for part in (first, second):
+        for part in halves:
             look_up_stay(3, part, stays[3][:, part])
 
-        differ(1, y1)
-        differ(2, y2)
-        terms = sbuf.tile([P, S], F32, name="terms")
-        news = [sbuf.tile([P, S], F32, name="news%d" % t) for t in range(TILES)]
-        old3a = sbuf.tile([P, S // 2], F32, name="old3a", tag="logs1", align_bytes=ALIGN)[:]
-        old3b = stays[1][:, first]
-        weigh(1, whole, stays[1][:], terms[:])
-        nc.vector.tensor_copy(old3a, states[3][:].indirect(entries(first)))
-        nc.vector.tensor_tensor(news[1][:], terms[:], y1, ALU.add)
-        nc.vector.tensor_copy(old3b, states[3][:].indirect(entries(second)))
-        nc.gpsimd.tensor_tensor(terms[:], stays[2][:], diffs[2][:], ALU.mult)
-        nc.gpsimd.tensor_tensor(news[2][:], terms[:], y2, ALU.add)
-        diff3 = y2
-        for part, old in ((first, old3a), (second, old3b)):
-            nc.gpsimd.tensor_tensor(diff3[:, part], old, y3[:, part], ALU.subtract)
-        for part in (first, second):
-            nc.gpsimd.tensor_tensor(terms[:, part], stays[3][:, part], diff3[:, part], ALU.mult)
+        diff = sbuf.tile([P, S], F32, name="diff")
+        terms = {t: sbuf.tile([P, S], F32, name="terms%d" % t) for t in (1, 2)}
+        news = {t: sbuf.tile([P, S], F32, name="news%d" % t) for t in (1, 2)}
+        for part in halves:
+            nc.vector.tensor_tensor(diff[:, part], states[1][:].indirect(entries(part)), y1[:, part], ALU.subtract)
+        few, most = slice(0, S - SHARE), slice(S - SHARE, S)
+        nc.vector.tensor_tensor(terms[1][:, few], stays[1][:, few], diff[:, few], ALU.mult)
+        nc.gpsimd.tensor_tensor(terms[1][:, most], stays[1][:, most], diff[:, most], ALU.mult)
+        nc.vector.tensor_copy(old3, states[3][:].indirect(tracks[:]))
+        nc.vector.tensor_tensor(news[1][:], terms[1][:], banks[1][:], ALU.subtract)
+        nc.vector.tensor_tensor(diff[:], states[2][:].indirect(tracks[:]), y2, ALU.subtract)
+        nc.gpsimd.tensor_tensor(terms[2][:], stays[2][:], diff[:], ALU.mult)
+        nc.gpsimd.tensor_tensor(news[2][:], terms[2][:], y2, ALU.add)
+        diff3 = sbuf.tile([P, S], F32, name="diff3", tag="variances3", align_bytes=ALIGN)
+        nc.gpsimd.tensor_tensor(diff3[:], old3, y3, ALU.subtract)
+        for part in halves:
+            nc.gpsimd.tensor_tensor(terms[1][:, part], stays[3][:, part], diff3[:, part], ALU.mult)
         for t in (1, 2):
             nc.vector.tensor_copy(states[t][:].indirect(tracks[:]), news[t][:])
             store(t)
-        scatter(3, whole, terms[:], y3)
+        scatter(3, whole, terms[1][:], y3)
         store(3)

@@ -22,7 +22,7 @@ GROUP = 16
 QUADRANT = 32
 SCALE_ROWS = 4
 SPREAD = QUADRANT // SCALE_ROWS
-SHARE = 384
+SHARE = 320
 ALIGN = 64
 
 
@@ -61,8 +61,10 @@ def tile_picked_kalman8_none_p_kernel(tc, x_words, x_scales, w1, st, va, offs, t
         nc.vector.tensor_copy(picked_bytes[:], all_scales[:].indirect(offsets[:]))
         for row in range(SCALE_ROWS):
             nc.sync.dma_start(x_bytes[row:P:QUADRANT, :].bitcast(I32), picked_bytes[SPREAD * row : P : QUADRANT, :].bitcast(I32))
+        left, right = slice(0, U // 2), slice(U // 2, U)
         for t in (1, 2):
-            nc.sync.dma_start(variances[t][:], va_rows[t])
+            for cols in (left, right):
+                nc.sync.dma_start(variances[t][:, cols], va_rows[t][:, cols])
         for t in (3, 1, 2):
             nc.sync.dma_start(states[t][:], st_rows[t])
         nc.sync.dma_start(variances[3][:], va_rows[3])
@@ -77,8 +79,8 @@ def tile_picked_kalman8_none_p_kernel(tc, x_words, x_scales, w1, st, va, offs, t
         def entries(part):
             return tracks[:, part.start // GROUP : part.stop // GROUP]
 
-        def logarithm(t):
-            nc.scalar.activation(logs[t][:], variances[t][:], ACT.Ln, bias=1.0, scale=2.0)
+        def logarithm(t, cols=slice(0, U)):
+            nc.scalar.activation(logs[t][:, cols], variances[t][:, cols], ACT.Ln, bias=1.0, scale=2.0)
 
         def look_up_stay(t, part, stay):
             nc.scalar.activation(stay, logs[t][:].indirect(entries(part)), ACT.Exp, scale=-1.0)
@@ -129,11 +131,13 @@ def tile_picked_kalman8_none_p_kernel(tc, x_words, x_scales, w1, st, va, offs, t
         store(0)
 
         halves = (first, second)
-        logarithm(1)
+        for cols in (left, right):
+            logarithm(1, cols)
         y1_old3 = sbuf.tile([P, S + S // 2], F32, name="y1_old3", tag="variances1", align_bytes=ALIGN)
         old3, y1 = y1_old3[:, :S], y1_old3[:, S // 2 :]
         nc.scalar.activation(y1, banks[1][:], ACT.Copy, scale=-1.0)
-        logarithm(2)
+        for cols in (left, right):
+            logarithm(2, cols)
         look_up_stay(1, whole, stays[1][:])
         look_up_stay(2, whole, stays[2][:])
         y2 = sbuf.tile([P, S], F32, name="y2", tag="logs1", align_bytes=ALIGN)[:]

@@ -61,38 +61,45 @@ def tile_picked_kalman8_none_p_kernel(tc, x_words, x_scales, w1, st, va, offs, t
         nc.vector.tensor_copy(picked_bytes[:], all_scales[:].indirect(offsets[:]))
         for row in range(SCALE_ROWS):
             nc.sync.dma_start(x_bytes[row:P:QUADRANT, :].bitcast(I32), picked_bytes[SPREAD * row : P : QUADRANT, :].bitcast(I32))
-        left, right = slice(0, U // 2), slice(U // 2, U)
-        for t in (1, 2):
-            for cols in (left, right):
-                nc.sync.dma_start(variances[t][:, cols], va_rows[t][:, cols])
-        for t in (3, 1, 2):
+        for t in (1, 2, 3):
+            nc.sync.dma_start(variances[t][:], va_rows[t])
             nc.sync.dma_start(states[t][:], st_rows[t])
-        nc.sync.dma_start(variances[3][:], va_rows[3])
 
         x_codes = sbuf.tile([P, S], U32, name="x_codes", align_bytes=ALIGN)
         banks = [psum.tile([P, S], F32, name="bank%d" % t) for t in range(TILES)]
-        logs = [sbuf.tile([P, U], F32, name="logs%d" % t, tag="logs%d" % t, align_bytes=ALIGN) for t in range(TILES)]
-        stays = [sbuf.tile([P, S], F32, name="keeps%d" % t) for t in range(TILES)]
-
-        whole, first, second = slice(0, S), slice(0, S // 2), slice(S // 2, S)
+        half = S // 2
+        whole, first, second = slice(0, S), slice(0, half), slice(half, S)
+        halves = (first, second)
 
         def entries(part):
             return tracks[:, part.start // GROUP : part.stop // GROUP]
 
-        def logarithm(t, cols=slice(0, U)):
-            nc.scalar.activation(logs[t][:, cols], variances[t][:, cols], ACT.Ln, bias=1.0, scale=2.0)
-
-        def look_up_stay(t, part, stay):
-            nc.scalar.activation(stay, logs[t][:].indirect(entries(part)), ACT.Exp, scale=-1.0)
-
-        def scatter(t, part, term, other):
-            nc.vector.tensor_tensor(states[t][:].indirect(entries(part)), term, other, ALU.add)
-
         def store(t):
             nc.sync.dma_start(out_rows[t], states[t][:])
 
-        logarithm(0)
-        look_up_stay(0, whole, stays[0][:])
+        kepts = [sbuf.tile([P, half], F32, name="kept%d" % t) for t in range(TILES - 1)]
+        terms = [sbuf.tile([P, 3 * half], F32, name="terms%d" % t) for t in range(TILES - 1)]
+        looked = [sbuf.tile([P, S], F32, name="looked%d" % t) for t in range(TILES)]
+        roots = [sbuf.tile([P, S], F32, name="roots%d" % t) for t in range(TILES)]
+        news = [sbuf.tile([P, half], F32, name="news%d" % t) for t in range(TILES - 1)]
+        stay0 = sbuf.tile([P, S], F32, name="stay0")
+        kept3 = sbuf.tile([P, S], F32, name="kept_last")
+        gained3 = sbuf.tile([P, S], F32, name="gained3")
+        stays = [stay0[:]] + [terms[t][:, :S] for t in range(TILES - 1)]
+
+        def kept(t, part):
+            return kepts[t][:]
+
+        def gained(t, part):
+            return terms[t][:, half + part.start : half + part.stop]
+
+        def new(t, part):
+            return news[t][:] if part == first else roots[t + 1][:, first]
+
+        roots_all = sbuf.tile([P, U], F32, name="roots_all")
+        nc.scalar.activation(roots_all[:], variances[0][:], ACT.Abs_reciprocal_sqrt, bias=1.0, scale=2.0)
+        nc.scalar.activation(roots[0][:], roots_all[:].indirect(tracks[:]), ACT.Copy)
+        nc.scalar.activation(stay0[:], roots[0][:], ACT.Square)
 
         pairs = (slice(0, 2), slice(2, 4))
         grouped = [sbuf.tile([P, 2, P, PACK], BF16, name="grouped%d" % h, align_bytes=ALIGN) for h in range(2)]
@@ -109,64 +116,69 @@ def tile_picked_kalman8_none_p_kernel(tc, x_words, x_scales, w1, st, va, offs, t
             nc.vector.quantize_mx(
                 out=w_codes[:, cols].bitcast(FP8X4), scales=w_bytes[:, cols], in_=grouped[h][:].rearrange("p t m j -> p (t m j)")
             )
-        nc.vector.tensor_copy(x_codes[:], all_words[:].bitcast(U32).indirect(offsets[:]))
+        for part in halves:
+            nc.vector.tensor_copy(x_codes[:, part], all_words[:].bitcast(U32).indirect(offsets[:, part.start // GROUP : part.stop // GROUP]))
 
-        kept0 = sbuf.tile([P, S], F32, name="kept0")
-        for part in (first, second):
-            nc.vector.tensor_tensor(kept0[:, part], states[0][:].indirect(entries(part)), stays[0][:, part], ALU.mult)
-        for t in range(TILES):
+        def product(t, part):
             cols = slice(P * t, P * (t + 1))
             nc.tensor.matmul_mx(
-                out=banks[t][:],
+                out=banks[t][:, part],
                 lhsT=w_codes[:, cols].bitcast(FP8X4),
                 lhsT_scale=w_bytes[:, cols],
-                rhs=x_codes[:].bitcast(FP8X4),
-                rhs_scale=x_bytes[:],
+                rhs=x_codes[:, part].bitcast(FP8X4),
+                rhs_scale=x_bytes[:, part],
                 start=True,
                 stop=True,
             )
-        for part in (first, second):
-            nc.vector.scalar_tensor_tensor(stays[0][:, part], stays[0][:, part], -1.0, banks[0][:, part], ALU.add, ALU.mult)
-        scatter(0, whole, kept0[:], stays[0][:])
-        store(0)
 
-        halves = (first, second)
-        for cols in (left, right):
-            logarithm(1, cols)
-        y1_old3 = sbuf.tile([P, S + S // 2], F32, name="y1_old3", tag="variances1", align_bytes=ALIGN)
-        old3, y1 = y1_old3[:, :S], y1_old3[:, S // 2 :]
-        nc.scalar.activation(y1, banks[1][:], ACT.Copy, scale=-1.0)
-        for cols in (left, right):
-            logarithm(2, cols)
-        look_up_stay(1, whole, stays[1][:])
-        look_up_stay(2, whole, stays[2][:])
-        y2 = sbuf.tile([P, S], F32, name="y2", tag="logs1", align_bytes=ALIGN)[:]
-        nc.scalar.activation(y2, banks[2][:], ACT.Copy, scale=-1.0)
-        y3 = sbuf.tile([P, S], F32, name="y3", tag="variances2", align_bytes=ALIGN)[:]
-        nc.scalar.activation(y3, banks[3][:], ACT.Copy, scale=-1.0)
-        logarithm(3)
-        for part in halves:
-            look_up_stay(3, part, stays[3][:, part])
+        def gain(t, out_ap, part):
+            nc.vector.scalar_tensor_tensor(out_ap, stays[t][:, part], -1.0, banks[t][:, part], ALU.add, ALU.mult)
 
-        diff = sbuf.tile([P, S], F32, name="diff")
-        terms = {t: sbuf.tile([P, S], F32, name="terms%d" % t) for t in (1, 2)}
-        news = {t: sbuf.tile([P, S], F32, name="news%d" % t) for t in (1, 2)}
+        def scatter(t, part):
+            nc.vector.tensor_copy(states[t][:].indirect(entries(part)), new(t, part))
+
+        def look_up_stay(t):
+            for part in halves:
+                nc.scalar.activation(looked[t][:, part], variances[t][:].indirect(entries(part)), ACT.Copy)
+            for part in halves:
+                nc.scalar.activation(roots[t][:, part], looked[t][:, part], ACT.Abs_reciprocal_sqrt, bias=1.0, scale=2.0)
+            for part in halves:
+                nc.scalar.activation(stays[t][:, part], roots[t][:, part], ACT.Square)
+
+        def look_up_state(t, part):
+            nc.scalar.activation(looked[t][:, part], states[t][:].indirect(entries(part)), ACT.Copy)
+
+        def keep(t, part):
+            nc.gpsimd.tensor_tensor(kept(t, part), stays[t][:, part], looked[t][:, part], ALU.mult)
+
+        def total(t, part):
+            nc.gpsimd.tensor_tensor(new(t, part), kept(t, part), gained(t, part), ALU.add)
+
         for part in halves:
-            nc.vector.tensor_tensor(diff[:, part], states[1][:].indirect(entries(part)), y1[:, part], ALU.subtract)
-        few, most = slice(0, S - SHARE), slice(S - SHARE, S)
-        nc.vector.tensor_tensor(terms[1][:, few], stays[1][:, few], diff[:, few], ALU.mult)
-        nc.gpsimd.tensor_tensor(terms[1][:, most], stays[1][:, most], diff[:, most], ALU.mult)
-        nc.vector.tensor_copy(old3, states[3][:].indirect(tracks[:]))
-        nc.vector.tensor_tensor(news[1][:], terms[1][:], banks[1][:], ALU.subtract)
-        nc.vector.tensor_tensor(diff[:], states[2][:].indirect(tracks[:]), y2, ALU.subtract)
-        nc.gpsimd.tensor_tensor(terms[2][:], stays[2][:], diff[:], ALU.mult)
-        nc.gpsimd.tensor_tensor(news[2][:], terms[2][:], y2, ALU.add)
-        diff3 = sbuf.tile([P, S], F32, name="diff3", tag="variances3", align_bytes=ALIGN)
-        nc.gpsimd.tensor_tensor(diff3[:], old3, y3, ALU.subtract)
+            product(0, part)
+        for t in range(1, TILES):
+            product(t, whole)
+        look_up_state(0, second)
+        nc.vector.tensor_tensor(kept(0, first), states[0][:].indirect(entries(first)), stay0[:, first], ALU.mult)
         for part in halves:
-            nc.gpsimd.tensor_tensor(terms[1][:, part], stays[3][:, part], diff3[:, part], ALU.mult)
-        for t in (1, 2):
-            nc.vector.tensor_copy(states[t][:].indirect(tracks[:]), news[t][:])
-            store(t)
-        scatter(3, whole, terms[1][:], y3)
+            gain(0, gained(0, part), part)
+        nc.vector.tensor_tensor(new(0, first), kept(0, first), gained(0, first), ALU.add)
+        keep(0, second)
+        scatter(0, first)
+        for t in range(1, TILES):
+            look_up_stay(t)
+            total(t - 1, second)
+            gain(t, gained(t, whole) if t < TILES - 1 else gained3[:], whole)
+            scatter(t - 1, second)
+            store(t - 1)
+            for part in halves:
+                look_up_state(t, part)
+            if t < TILES - 1:
+                keep(t, first)
+                total(t, first)
+                keep(t, second)
+                scatter(t, first)
+        for part in halves:
+            nc.gpsimd.tensor_tensor(kept3[:, part], stays[3][:, part], looked[3][:, part], ALU.mult)
+        nc.vector.tensor_tensor(states[3][:].indirect(tracks[:]), kept3[:], gained3[:], ALU.add)
         store(3)

@@ -67,6 +67,7 @@ def tile_picked_kalman8_none_p_kernel(tc, x_words, x_scales, w1, st, va, offs, t
 
         x_codes = sbuf.tile([P, S], U32, name="x_codes", align_bytes=ALIGN)
         banks = [psum.tile([P, S], F32, name="bank%d" % t) for t in range(TILES)]
+        late_bank = psum.tile([P, S], F32, name="late_bank")
         half = S // 2
         whole, first, second = slice(0, S), slice(0, half), slice(half, S)
         halves = (first, second)
@@ -85,16 +86,20 @@ def tile_picked_kalman8_none_p_kernel(tc, x_words, x_scales, w1, st, va, offs, t
         stay0 = sbuf.tile([P, S], F32, name="stay0")
         kept3 = sbuf.tile([P, S], F32, name="kept_last")
         gained3 = sbuf.tile([P, S], F32, name="gained3")
-        stays = [stay0[:]] + [terms[t][:, :S] for t in range(TILES - 1)]
+        stay1 = sbuf.tile([P, S], F32, name="stay1")
+        stays = [stay0[:], stay1[:]] + [terms[t][:, half:] for t in range(1, TILES - 1)]
+        olds = [sbuf.tile([P, S], F32, name="olds%d" % t) for t in range(TILES)]
 
         def kept(t, part):
-            return kepts[t][:]
+            return news[0][:] if (t, part) == (0, first) else kepts[t][:]
 
         def gained(t, part):
-            return terms[t][:, half + part.start : half + part.stop]
+            return terms[t][:, half : 2 * half] if part == first else terms[t][:, :half]
 
         def new(t, part):
-            return news[t][:] if part == first else roots[t + 1][:, first]
+            if part == first:
+                return news[t][:]
+            return looked[t + 1][:, second] if t < TILES - 2 else roots[t + 1][:, first]
 
         roots_all = sbuf.tile([P, U], F32, name="roots_all")
         nc.scalar.activation(roots_all[:], variances[0][:], ACT.Abs_reciprocal_sqrt, bias=1.0, scale=2.0)
@@ -119,10 +124,13 @@ def tile_picked_kalman8_none_p_kernel(tc, x_words, x_scales, w1, st, va, offs, t
         for part in halves:
             nc.vector.tensor_copy(x_codes[:, part], all_words[:].bitcast(U32).indirect(offsets[:, part.start // GROUP : part.stop // GROUP]))
 
+        def bank(t, part):
+            return late_bank[:, part] if (t, part) == (0, second) else banks[t][:, part]
+
         def product(t, part):
             cols = slice(P * t, P * (t + 1))
             nc.tensor.matmul_mx(
-                out=banks[t][:, part],
+                out=bank(t, part),
                 lhsT=w_codes[:, cols].bitcast(FP8X4),
                 lhsT_scale=w_bytes[:, cols],
                 rhs=x_codes[:, part].bitcast(FP8X4),
@@ -132,27 +140,29 @@ def tile_picked_kalman8_none_p_kernel(tc, x_words, x_scales, w1, st, va, offs, t
             )
 
         def gain(t, out_ap, part):
-            nc.vector.scalar_tensor_tensor(out_ap, stays[t][:, part], -1.0, banks[t][:, part], ALU.add, ALU.mult)
+            nc.vector.scalar_tensor_tensor(out_ap, stays[t][:, part], -1.0, bank(t, part), ALU.add, ALU.mult)
 
         def scatter(t, part):
             nc.vector.tensor_copy(states[t][:].indirect(entries(part)), new(t, part))
 
-        def look_up_stay(t):
+        def look_up_root(t):
             for part in halves:
                 nc.scalar.activation(looked[t][:, part], variances[t][:].indirect(entries(part)), ACT.Copy)
             for part in halves:
                 nc.scalar.activation(roots[t][:, part], looked[t][:, part], ACT.Abs_reciprocal_sqrt, bias=1.0, scale=2.0)
-            for part in halves:
-                nc.scalar.activation(stays[t][:, part], roots[t][:, part], ACT.Square)
+
+        def square(t, part):
+            nc.scalar.activation(stays[t][:, part], roots[t][:, part], ACT.Square)
 
         def look_up_state(t, part):
-            nc.scalar.activation(looked[t][:, part], states[t][:].indirect(entries(part)), ACT.Copy)
+            nc.scalar.activation(olds[t][:, part], states[t][:].indirect(entries(part)), ACT.Copy)
 
         def keep(t, part):
-            nc.gpsimd.tensor_tensor(kept(t, part), stays[t][:, part], looked[t][:, part], ALU.mult)
+            nc.gpsimd.tensor_tensor(kept(t, part), stays[t][:, part], olds[t][:, part], ALU.mult)
 
         def total(t, part):
-            nc.gpsimd.tensor_tensor(new(t, part), kept(t, part), gained(t, part), ALU.add)
+            engine = nc.vector if t == 0 else nc.gpsimd
+            engine.tensor_tensor(new(t, part), kept(t, part), gained(t, part), ALU.add)
 
         for part in halves:
             product(0, part)
@@ -162,23 +172,33 @@ def tile_picked_kalman8_none_p_kernel(tc, x_words, x_scales, w1, st, va, offs, t
         nc.vector.tensor_tensor(kept(0, first), states[0][:].indirect(entries(first)), stay0[:, first], ALU.mult)
         for part in halves:
             gain(0, gained(0, part), part)
-        nc.vector.tensor_tensor(new(0, first), kept(0, first), gained(0, first), ALU.add)
         keep(0, second)
-        scatter(0, first)
-        for t in range(1, TILES):
-            look_up_stay(t)
+        nc.vector.tensor_tensor(states[0][:].indirect(entries(first)), kept(0, first), gained(0, first), ALU.add)
+        for t in range(1, TILES - 1):
+            look_up_root(t)
             total(t - 1, second)
-            gain(t, gained(t, whole) if t < TILES - 1 else gained3[:], whole)
+            square(t, first)
+            gain(t, gained(t, first), first)
             scatter(t - 1, second)
             store(t - 1)
-            for part in halves:
-                look_up_state(t, part)
-            if t < TILES - 1:
-                keep(t, first)
-                total(t, first)
-                keep(t, second)
-                scatter(t, first)
+            look_up_state(t, first)
+            square(t, second)
+            look_up_state(t, second)
+            gain(t, gained(t, second), second)
+            keep(t, first)
+            total(t, first)
+            keep(t, second)
+            scatter(t, first)
+        look_up_root(3)
         for part in halves:
-            nc.gpsimd.tensor_tensor(kept3[:, part], stays[3][:, part], looked[3][:, part], ALU.mult)
+            square(3, part)
+        total(2, second)
+        gain(3, gained3[:], whole)
+        scatter(2, second)
+        store(2)
+        for part in halves:
+            look_up_state(3, part)
+        for part in halves:
+            nc.gpsimd.tensor_tensor(kept3[:, part], stays[3][:, part], olds[3][:, part], ALU.mult)
         nc.vector.tensor_tensor(states[3][:].indirect(tracks[:]), kept3[:], gained3[:], ALU.add)
         store(3)

@@ -61,9 +61,11 @@ def tile_picked_kalman8_none_p_kernel(tc, x_words, x_scales, w1, st, va, offs, t
         nc.vector.tensor_copy(picked_bytes[:], all_scales[:].indirect(offsets[:]))
         for row in range(SCALE_ROWS):
             nc.sync.dma_start(x_bytes[row:P:QUADRANT, :].bitcast(I32), picked_bytes[SPREAD * row : P : QUADRANT, :].bitcast(I32))
-        for t in (1, 2, 3):
+        for t in (1, 2):
             nc.sync.dma_start(variances[t][:], va_rows[t])
             nc.sync.dma_start(states[t][:], st_rows[t])
+        nc.sync.dma_start(states[3][:], st_rows[3])
+        nc.sync.dma_start(variances[3][:], va_rows[3])
 
         x_codes = sbuf.tile([P, S], U32, name="x_codes", align_bytes=ALIGN)
         banks = [psum.tile([P, S], F32, name="bank%d" % t) for t in range(TILES)]
@@ -78,7 +80,7 @@ def tile_picked_kalman8_none_p_kernel(tc, x_words, x_scales, w1, st, va, offs, t
         def store(t):
             nc.sync.dma_start(out_rows[t], states[t][:])
 
-        kepts = [sbuf.tile([P, half], F32, name="kept%d" % t) for t in range(TILES - 1)]
+        kepts = [sbuf.tile([P, S], F32, name="kept%d" % t) for t in range(TILES - 1)]
         terms = [sbuf.tile([P, 3 * half], F32, name="terms%d" % t) for t in range(TILES - 1)]
         looked = [sbuf.tile([P, S], F32, name="looked%d" % t) for t in range(TILES)]
         roots = [sbuf.tile([P, S], F32, name="roots%d" % t) for t in range(TILES)]
@@ -91,7 +93,7 @@ def tile_picked_kalman8_none_p_kernel(tc, x_words, x_scales, w1, st, va, offs, t
         olds = [sbuf.tile([P, S], F32, name="olds%d" % t) for t in range(TILES)]
 
         def kept(t, part):
-            return news[0][:] if (t, part) == (0, first) else kepts[t][:]
+            return kepts[t][:, part]
 
         def gained(t, part):
             return terms[t][:, half : 2 * half] if part == first else terms[t][:, :half]
@@ -99,7 +101,7 @@ def tile_picked_kalman8_none_p_kernel(tc, x_words, x_scales, w1, st, va, offs, t
         def new(t, part):
             if part == first:
                 return news[t][:]
-            return looked[t + 1][:, second] if t < TILES - 2 else roots[t + 1][:, first]
+            return looked[t + 1][:, second] if t < TILES - 2 else variances[3][:, S : S + half]
 
         roots_all = sbuf.tile([P, U], F32, name="roots_all")
         nc.scalar.activation(roots_all[:], variances[0][:], ACT.Abs_reciprocal_sqrt, bias=1.0, scale=2.0)
@@ -189,16 +191,24 @@ def tile_picked_kalman8_none_p_kernel(tc, x_words, x_scales, w1, st, va, offs, t
             total(t, first)
             keep(t, second)
             scatter(t, first)
-        look_up_root(3)
+        old3 = variances[3][:, :S]
+        doubled = roots[2][:, second]
         for part in halves:
-            square(3, part)
+            nc.scalar.activation(looked[3][:, part], variances[3][:].indirect(entries(part)), ACT.Copy)
+        for part in halves:
+            nc.scalar.activation(old3[:, part], states[3][:].indirect(entries(part)), ACT.Copy)
+        nc.scalar.activation(doubled, banks[3][:, second], ACT.Copy, scale=-2.0)
+        for part in halves:
+            nc.scalar.activation(roots[3][:, part], looked[3][:, part], ACT.Abs_reciprocal_sqrt, bias=1.0, scale=2.0)
+        for part in halves:
+            nc.scalar.activation(kept3[:, part], roots[3][:, part], ACT.Square)
+        mixed_first, mixed_second = terms[2][:, half : 2 * half], terms[2][:, 2 * half :]
         total(2, second)
-        gain(3, gained3[:], whole)
+        nc.vector.scalar_tensor_tensor(mixed_first, looked[3][:, first], -2.0, banks[3][:, first], ALU.mult, ALU.mult)
         scatter(2, second)
         store(2)
-        for part in halves:
-            look_up_state(3, part)
-        for part in halves:
-            nc.gpsimd.tensor_tensor(kept3[:, part], stays[3][:, part], olds[3][:, part], ALU.mult)
-        nc.vector.tensor_tensor(states[3][:].indirect(tracks[:]), kept3[:], gained3[:], ALU.add)
+        nc.gpsimd.tensor_tensor(mixed_second, looked[3][:, second], doubled, ALU.mult)
+        nc.gpsimd.tensor_tensor(gained3[:, first], old3[:, first], mixed_first, ALU.add)
+        nc.gpsimd.tensor_tensor(gained3[:, second], old3[:, second], mixed_second, ALU.add)
+        nc.vector.tensor_tensor(states[3][:].indirect(tracks[:]), kept3[:], gained3[:], ALU.mult)
         store(3)

@@ -18,11 +18,13 @@ ACT = mybir.ActivationFunctionType
 P = 128
 PACK = 4
 TILES = N // P
+LAST = TILES - 1
+HALF = S // 2
 GROUP = 16
 QUADRANT = 32
 SCALE_ROWS = 4
 SPREAD = QUADRANT // SCALE_ROWS
-SHARE = 320
+SHARE = 192
 ALIGN = 64
 
 
@@ -42,9 +44,7 @@ def tile_picked_kalman8_none_p_kernel(tc, x_words, x_scales, w1, st, va, offs, t
         all_words = sbuf.tile([P, T], I32, name="all_words", align_bytes=ALIGN)
         w_raw = sbuf.tile([P, PACK, N], F32, name="w_raw")
         states = [sbuf.tile([P, U], F32, name="states%d" % t) for t in range(TILES)]
-        variances = [
-            sbuf.tile([P, U], F32, name="variances%d" % t, tag="variances%d" % t, align_bytes=ALIGN) for t in range(TILES)
-        ]
+        variances = [sbuf.tile([P, U], F32, name="variances%d" % t) for t in range(TILES)]
 
         nc.vector.memset(all_scales[:].bitcast(I32), 0)
 
@@ -61,52 +61,51 @@ def tile_picked_kalman8_none_p_kernel(tc, x_words, x_scales, w1, st, va, offs, t
         nc.vector.tensor_copy(picked_bytes[:], all_scales[:].indirect(offsets[:]))
         for row in range(SCALE_ROWS):
             nc.sync.dma_start(x_bytes[row:P:QUADRANT, :].bitcast(I32), picked_bytes[SPREAD * row : P : QUADRANT, :].bitcast(I32))
-        for t in (1, 2):
+        for t in range(1, LAST):
             nc.sync.dma_start(variances[t][:], va_rows[t])
             nc.sync.dma_start(states[t][:], st_rows[t])
-        nc.sync.dma_start(states[3][:], st_rows[3])
-        nc.sync.dma_start(variances[3][:], va_rows[3])
+        nc.sync.dma_start(states[LAST][:], st_rows[LAST])
+        nc.sync.dma_start(variances[LAST][:], va_rows[LAST])
+
+        whole, first, second = slice(0, S), slice(0, HALF), slice(HALF, S)
+        halves = (first, second)
+
+        def columns(part):
+            return slice(part.start // GROUP, part.stop // GROUP)
 
         x_codes = sbuf.tile([P, S], U32, name="x_codes", align_bytes=ALIGN)
         banks = [psum.tile([P, S], F32, name="bank%d" % t) for t in range(TILES)]
         late_bank = psum.tile([P, S], F32, name="late_bank")
-        half = S // 2
-        whole, first, second = slice(0, S), slice(0, half), slice(half, S)
-        halves = (first, second)
-
-        def entries(part):
-            return tracks[:, part.start // GROUP : part.stop // GROUP]
-
-        def store(t):
-            nc.sync.dma_start(out_rows[t], states[t][:])
-
-        kepts = [sbuf.tile([P, S], F32, name="kept%d" % t) for t in range(TILES - 1)]
-        terms = [sbuf.tile([P, 3 * half], F32, name="terms%d" % t) for t in range(TILES - 1)]
-        looked = [sbuf.tile([P, S], F32, name="looked%d" % t) for t in range(TILES)]
+        picked = {t: sbuf.tile([P, S], F32, name="picked%d" % t) for t in range(1, TILES)}
+        olds = [sbuf.tile([P, S], F32, name="olds%d" % t) for t in range(LAST)]
         roots = [sbuf.tile([P, S], F32, name="roots%d" % t) for t in range(TILES)]
-        news = [sbuf.tile([P, half], F32, name="news%d" % t) for t in range(TILES - 1)]
-        stay0 = sbuf.tile([P, S], F32, name="stay0")
-        kept3 = sbuf.tile([P, S], F32, name="kept_last")
-        gained3 = sbuf.tile([P, S], F32, name="gained3")
-        stay1 = sbuf.tile([P, S], F32, name="stay1")
-        stays = [stay0[:], stay1[:]] + [terms[t][:, half:] for t in range(1, TILES - 1)]
-        olds = [sbuf.tile([P, S], F32, name="olds%d" % t) for t in range(TILES)]
+
+        kepts = [sbuf.tile([P, S], F32, name="kept%d" % t) for t in range(LAST)]
+        terms = [sbuf.tile([P, 2 * HALF if t == 0 else 3 * HALF], F32, name="terms%d" % t) for t in range(LAST)]
+        news_first = {t: sbuf.tile([P, HALF], F32, name="new_first%d" % t) for t in range(1, LAST)}
+        news_second = [picked[1][:, second], picked[2][:, second], variances[LAST][:, S : S + HALF]]
+        stays = [sbuf.tile([P, S], F32, name="stay%d" % t)[:] for t in range(2)]
+        stays.extend([terms[1][:, HALF:], sbuf.tile([P, S], F32, name="stay_last")[:]])
+
+        def bank(t, part):
+            return late_bank[:, part] if (t, part) == (0, second) else banks[t][:, part]
 
         def kept(t, part):
             return kepts[t][:, part]
 
         def gained(t, part):
-            return terms[t][:, half : 2 * half] if part == first else terms[t][:, :half]
+            return terms[t][:, HALF : 2 * HALF] if part == first else terms[t][:, :HALF]
 
         def new(t, part):
-            if part == first:
-                return news[t][:]
-            return looked[t + 1][:, second] if t < TILES - 2 else variances[3][:, S : S + half]
+            return news_first[t][:] if part == first else news_second[t]
+
+        def window(tile, part):
+            return tile[:].indirect(tracks[:, columns(part)])
 
         roots_all = sbuf.tile([P, U], F32, name="roots_all")
         nc.scalar.activation(roots_all[:], variances[0][:], ACT.Abs_reciprocal_sqrt, bias=1.0, scale=2.0)
-        nc.scalar.activation(roots[0][:], roots_all[:].indirect(tracks[:]), ACT.Copy)
-        nc.scalar.activation(stay0[:], roots[0][:], ACT.Square)
+        nc.scalar.activation(roots[0][:], window(roots_all, whole), ACT.Copy)
+        nc.scalar.activation(stays[0], roots[0][:], ACT.Square)
 
         pairs = (slice(0, 2), slice(2, 4))
         grouped = [sbuf.tile([P, 2, P, PACK], BF16, name="grouped%d" % h, align_bytes=ALIGN) for h in range(2)]
@@ -124,10 +123,7 @@ def tile_picked_kalman8_none_p_kernel(tc, x_words, x_scales, w1, st, va, offs, t
                 out=w_codes[:, cols].bitcast(FP8X4), scales=w_bytes[:, cols], in_=grouped[h][:].rearrange("p t m j -> p (t m j)")
             )
         for part in halves:
-            nc.vector.tensor_copy(x_codes[:, part], all_words[:].bitcast(U32).indirect(offsets[:, part.start // GROUP : part.stop // GROUP]))
-
-        def bank(t, part):
-            return late_bank[:, part] if (t, part) == (0, second) else banks[t][:, part]
+            nc.vector.tensor_copy(x_codes[:, part], all_words[:].bitcast(U32).indirect(offsets[:, columns(part)]))
 
         def product(t, part):
             cols = slice(P * t, P * (t + 1))
@@ -141,74 +137,82 @@ def tile_picked_kalman8_none_p_kernel(tc, x_words, x_scales, w1, st, va, offs, t
                 stop=True,
             )
 
-        def gain(t, out_ap, part):
-            nc.vector.scalar_tensor_tensor(out_ap, stays[t][:, part], -1.0, bank(t, part), ALU.add, ALU.mult)
-
-        def scatter(t, part):
-            nc.vector.tensor_copy(states[t][:].indirect(entries(part)), new(t, part))
-
-        def look_up_root(t):
+        def look_up_variances(t):
             for part in halves:
-                nc.scalar.activation(looked[t][:, part], variances[t][:].indirect(entries(part)), ACT.Copy)
+                nc.scalar.activation(picked[t][:, part], window(variances[t], part), ACT.Copy)
+
+        def root(t):
             for part in halves:
-                nc.scalar.activation(roots[t][:, part], looked[t][:, part], ACT.Abs_reciprocal_sqrt, bias=1.0, scale=2.0)
+                nc.scalar.activation(roots[t][:, part], picked[t][:, part], ACT.Abs_reciprocal_sqrt, bias=1.0, scale=2.0)
 
         def square(t, part):
             nc.scalar.activation(stays[t][:, part], roots[t][:, part], ACT.Square)
 
         def look_up_state(t, part):
-            nc.scalar.activation(olds[t][:, part], states[t][:].indirect(entries(part)), ACT.Copy)
+            nc.scalar.activation(olds[t][:, part], window(states[t], part), ACT.Copy)
+
+        def gain(t, part):
+            nc.vector.scalar_tensor_tensor(gained(t, part), stays[t][:, part], -1.0, bank(t, part), ALU.add, ALU.mult)
 
         def keep(t, part):
             nc.gpsimd.tensor_tensor(kept(t, part), stays[t][:, part], olds[t][:, part], ALU.mult)
 
-        def total(t, part):
-            engine = nc.vector if t == 0 else nc.gpsimd
+        def total(engine, t, part):
             engine.tensor_tensor(new(t, part), kept(t, part), gained(t, part), ALU.add)
+
+        def scatter(t, part):
+            nc.vector.tensor_copy(window(states[t], part), new(t, part))
+
+        def store(t):
+            nc.sync.dma_start(out_rows[t], states[t][:])
 
         for part in halves:
             product(0, part)
         for t in range(1, TILES):
             product(t, whole)
+
         look_up_state(0, second)
-        nc.vector.tensor_tensor(kept(0, first), states[0][:].indirect(entries(first)), stay0[:, first], ALU.mult)
+        nc.vector.tensor_tensor(kept(0, first), window(states[0], first), stays[0][:, first], ALU.mult)
         for part in halves:
-            gain(0, gained(0, part), part)
+            gain(0, part)
         keep(0, second)
-        nc.vector.tensor_tensor(states[0][:].indirect(entries(first)), kept(0, first), gained(0, first), ALU.add)
-        for t in range(1, TILES - 1):
-            look_up_root(t)
-            total(t - 1, second)
+        nc.vector.tensor_tensor(window(states[0], first), kept(0, first), gained(0, first), ALU.add)
+
+        for t in range(1, LAST):
+            look_up_variances(t)
+            root(t)
+            total(nc.vector if t == 1 else nc.gpsimd, t - 1, second)
             square(t, first)
-            gain(t, gained(t, first), first)
+            gain(t, first)
             scatter(t - 1, second)
             store(t - 1)
             look_up_state(t, first)
             square(t, second)
             look_up_state(t, second)
-            gain(t, gained(t, second), second)
+            gain(t, second)
             keep(t, first)
-            total(t, first)
+            total(nc.gpsimd, t, first)
             keep(t, second)
             scatter(t, first)
-        old3 = variances[3][:, :S]
-        doubled = roots[2][:, second]
+
+        most, few = slice(0, S - SHARE), slice(S - SHARE, S)
+        old_last = variances[LAST][:, :S]
+        doubled = roots[LAST - 1][:, few]
+        weighed = terms[LAST - 1][:, HALF:]
+        pooled = sbuf.tile([P, S], F32, name="pooled")
+        look_up_variances(LAST)
+        for part in (second, first):
+            nc.scalar.activation(old_last[:, part], window(states[LAST], part), ACT.Copy)
+        nc.scalar.activation(doubled, bank(LAST, few), ACT.Copy, scale=-2.0)
+        root(LAST)
         for part in halves:
-            nc.scalar.activation(looked[3][:, part], variances[3][:].indirect(entries(part)), ACT.Copy)
-        for part in halves:
-            nc.scalar.activation(old3[:, part], states[3][:].indirect(entries(part)), ACT.Copy)
-        nc.scalar.activation(doubled, banks[3][:, second], ACT.Copy, scale=-2.0)
-        for part in halves:
-            nc.scalar.activation(roots[3][:, part], looked[3][:, part], ACT.Abs_reciprocal_sqrt, bias=1.0, scale=2.0)
-        for part in halves:
-            nc.scalar.activation(kept3[:, part], roots[3][:, part], ACT.Square)
-        mixed_first, mixed_second = terms[2][:, half : 2 * half], terms[2][:, 2 * half :]
-        total(2, second)
-        nc.vector.scalar_tensor_tensor(mixed_first, looked[3][:, first], -2.0, banks[3][:, first], ALU.mult, ALU.mult)
-        scatter(2, second)
-        store(2)
-        nc.gpsimd.tensor_tensor(mixed_second, looked[3][:, second], doubled, ALU.mult)
-        nc.gpsimd.tensor_tensor(gained3[:, first], old3[:, first], mixed_first, ALU.add)
-        nc.gpsimd.tensor_tensor(gained3[:, second], old3[:, second], mixed_second, ALU.add)
-        nc.vector.tensor_tensor(states[3][:].indirect(tracks[:]), kept3[:], gained3[:], ALU.mult)
-        store(3)
+            square(LAST, part)
+        nc.gpsimd.tensor_tensor(weighed[:, few], picked[LAST][:, few], doubled, ALU.mult)
+        total(nc.gpsimd, LAST - 1, second)
+        nc.vector.scalar_tensor_tensor(weighed[:, most], picked[LAST][:, most], -2.0, bank(LAST, most), ALU.mult, ALU.mult)
+        scatter(LAST - 1, second)
+        store(LAST - 1)
+        for part in (few, most):
+            nc.gpsimd.tensor_tensor(pooled[:, part], old_last[:, part], weighed[:, part], ALU.add)
+        nc.vector.tensor_tensor(window(states[LAST], whole), stays[LAST], pooled[:], ALU.mult)
+        store(LAST)

from contextlib import ExitStack

import concourse.mybir as mybir

K, T, S, N, U = 512, 2048, 512, 512, 1024
FLOPS = 2 * K * N * S

F32 = mybir.dt.float32
BF16 = mybir.dt.bfloat16
I32 = mybir.dt.int32
U32 = mybir.dt.uint32
U16 = mybir.dt.uint16
U8 = mybir.dt.uint8
FP8X4 = mybir.dt.float8_e4m3fn_x4
ALU = mybir.AluOpType
ACT = mybir.ActivationFunctionType

P = 128
PACK = 4
TILES = N // P
LAST = TILES - 1
HALF = S // 2
GROUP = 16
QUADRANT = 32
SCALE_ROWS = 4
SPREAD = QUADRANT // SCALE_ROWS
SHARE = 192
ALIGN = 64


def tile_picked_kalman8_none_p_kernel(tc, x_words, x_scales, w1, st, va, offs, trk, out):
    nc = tc.nc
    with ExitStack() as ctx:
        sbuf = ctx.enter_context(tc.tile_pool(name="keep", bufs=1))
        psum = ctx.enter_context(tc.psum_pool(name="psum", bufs=1))

        st_rows = st.rearrange("(p t) u -> t p u", t=TILES)
        va_rows = va.rearrange("(p t) u -> t p u", t=TILES)
        out_rows = out.rearrange("(p t) u -> t p u", t=TILES)

        offsets = sbuf.tile([P, S // GROUP], U16, name="offsets")
        tracks = sbuf.tile([P, S // GROUP], U16, name="tracks")
        all_scales = sbuf.tile([P, T], U8, name="all_scales", align_bytes=ALIGN)
        all_words = sbuf.tile([P, T], I32, name="all_words", align_bytes=ALIGN)
        w_raw = sbuf.tile([P, PACK, N], F32, name="w_raw")
        states = [sbuf.tile([P, U], F32, name="states%d" % t) for t in range(TILES)]
        variances = [sbuf.tile([P, U], F32, name="variances%d" % t) for t in range(TILES)]

        nc.vector.memset(all_scales[:].bitcast(I32), 0)

        nc.sync.dma_start(variances[0][:], va_rows[0])
        nc.sync.dma_start(offsets[:], offs)
        nc.sync.dma_start(tracks[:], trk)
        nc.sync.dma_start(all_scales[0:P:SPREAD, :].bitcast(I32), x_scales[0].bitcast(I32))
        nc.sync.dma_start(w_raw[:], w1.rearrange("(p j) c -> p j c", j=PACK))
        nc.sync.dma_start(all_words[:], x_words[0].rearrange("p n r -> p (n r)").bitcast(I32))
        nc.sync.dma_start(states[0][:], st_rows[0])
        picked_bytes = sbuf.tile([P, S], U8, name="picked_bytes", align_bytes=ALIGN)
        x_bytes = sbuf.tile([P, S], U8, name="x_bytes", align_bytes=ALIGN)
        nc.vector.memset(x_bytes[:].bitcast(I32), 0)
        nc.vector.tensor_copy(picked_bytes[:], all_scales[:].indirect(offsets[:]))
        for row in range(SCALE_ROWS):
            nc.sync.dma_start(x_bytes[row:P:QUADRANT, :].bitcast(I32), picked_bytes[SPREAD * row : P : QUADRANT, :].bitcast(I32))
        for t in range(1, LAST):
            nc.sync.dma_start(variances[t][:], va_rows[t])
            nc.sync.dma_start(states[t][:], st_rows[t])
        nc.sync.dma_start(states[LAST][:], st_rows[LAST])
        nc.sync.dma_start(variances[LAST][:], va_rows[LAST])

        whole, first, second = slice(0, S), slice(0, HALF), slice(HALF, S)
        halves = (first, second)

        def columns(part):
            return slice(part.start // GROUP, part.stop // GROUP)

        x_codes = sbuf.tile([P, S], U32, name="x_codes", align_bytes=ALIGN)
        banks = [psum.tile([P, S], F32, name="bank%d" % t) for t in range(TILES)]
        late_bank = psum.tile([P, S], F32, name="late_bank")
        picked = {t: sbuf.tile([P, S], F32, name="picked%d" % t) for t in range(1, TILES)}
        olds = [sbuf.tile([P, S], F32, name="olds%d" % t) for t in range(LAST)]
        roots = [sbuf.tile([P, S], F32, name="roots%d" % t) for t in range(TILES)]

        kepts = [sbuf.tile([P, S], F32, name="kept%d" % t) for t in range(LAST)]
        terms = [sbuf.tile([P, 2 * HALF if t == 0 else 3 * HALF], F32, name="terms%d" % t) for t in range(LAST)]
        news_first = {t: sbuf.tile([P, HALF], F32, name="new_first%d" % t) for t in range(1, LAST)}
        news_second = [picked[1][:, second], picked[2][:, second], variances[LAST][:, S : S + HALF]]
        stays = [sbuf.tile([P, S], F32, name="stay%d" % t)[:] for t in range(2)]
        stays.extend([terms[1][:, HALF:], sbuf.tile([P, S], F32, name="stay_last")[:]])

        def bank(t, part):
            return late_bank[:, part] if (t, part) == (0, second) else banks[t][:, part]

        def kept(t, part):
            return kepts[t][:, part]

        def gained(t, part):
            return terms[t][:, HALF : 2 * HALF] if part == first else terms[t][:, :HALF]

        def new(t, part):
            return news_first[t][:] if part == first else news_second[t]

        def window(tile, part):
            return tile[:].indirect(tracks[:, columns(part)])

        roots_all = sbuf.tile([P, U], F32, name="roots_all")
        nc.scalar.activation(roots_all[:], variances[0][:], ACT.Abs_reciprocal_sqrt, bias=1.0, scale=2.0)
        nc.scalar.activation(roots[0][:], window(roots_all, whole), ACT.Copy)
        nc.scalar.activation(stays[0], roots[0][:], ACT.Square)

        pairs = (slice(0, 2), slice(2, 4))
        grouped = [sbuf.tile([P, 2, P, PACK], BF16, name="grouped%d" % h, align_bytes=ALIGN) for h in range(2)]
        for h in range(2):
            nc.vector.tensor_scalar_mul(
                grouped[h][:].rearrange("p t m j -> p m t j"),
                w_raw[:].rearrange("p j (m t) -> p m t j", t=TILES)[:, :, pairs[h], :],
                -1.0,
            )
        w_codes = sbuf.tile([P, N], U32, name="w_codes", align_bytes=ALIGN)
        w_bytes = sbuf.tile([P, N], U8, name="w_bytes", align_bytes=ALIGN)
        for h in range(2):
            cols = slice(2 * P * h, 2 * P * (h + 1))
            nc.vector.quantize_mx(
                out=w_codes[:, cols].bitcast(FP8X4), scales=w_bytes[:, cols], in_=grouped[h][:].rearrange("p t m j -> p (t m j)")
            )
        for part in halves:
            nc.vector.tensor_copy(x_codes[:, part], all_words[:].bitcast(U32).indirect(offsets[:, columns(part)]))

        def product(t, part):
            cols = slice(P * t, P * (t + 1))
            nc.tensor.matmul_mx(
                out=bank(t, part),
                lhsT=w_codes[:, cols].bitcast(FP8X4),
                lhsT_scale=w_bytes[:, cols],
                rhs=x_codes[:, part].bitcast(FP8X4),
                rhs_scale=x_bytes[:, part],
                start=True,
                stop=True,
            )

        def look_up_variances(t):
            for part in halves:
                nc.scalar.activation(picked[t][:, part], window(variances[t], part), ACT.Copy)

        def root(t):
            for part in halves:
                nc.scalar.activation(roots[t][:, part], picked[t][:, part], ACT.Abs_reciprocal_sqrt, bias=1.0, scale=2.0)

        def square(t, part):
            nc.scalar.activation(stays[t][:, part], roots[t][:, part], ACT.Square)

        def look_up_state(t, part):
            nc.scalar.activation(olds[t][:, part], window(states[t], part), ACT.Copy)

        def gain(t, part):
            nc.vector.scalar_tensor_tensor(gained(t, part), stays[t][:, part], -1.0, bank(t, part), ALU.add, ALU.mult)

        def keep(t, part):
            nc.gpsimd.tensor_tensor(kept(t, part), stays[t][:, part], olds[t][:, part], ALU.mult)

        def total(engine, t, part):
            engine.tensor_tensor(new(t, part), kept(t, part), gained(t, part), ALU.add)

        def scatter(t, part):
            nc.vector.tensor_copy(window(states[t], part), new(t, part))

        def store(t):
            nc.sync.dma_start(out_rows[t], states[t][:])

        for part in halves:
            product(0, part)
        for t in range(1, TILES):
            product(t, whole)

        look_up_state(0, second)
        nc.vector.tensor_tensor(kept(0, first), window(states[0], first), stays[0][:, first], ALU.mult)
        for part in halves:
            gain(0, part)
        keep(0, second)
        nc.vector.tensor_tensor(window(states[0], first), kept(0, first), gained(0, first), ALU.add)

        for t in range(1, LAST):
            look_up_variances(t)
            root(t)
            total(nc.vector if t == 1 else nc.gpsimd, t - 1, second)
            square(t, first)
            gain(t, first)
            scatter(t - 1, second)
            store(t - 1)
            look_up_state(t, first)
            square(t, second)
            look_up_state(t, second)
            gain(t, second)
            keep(t, first)
            total(nc.gpsimd, t, first)
            keep(t, second)
            scatter(t, first)

        most, few = slice(0, S - SHARE), slice(S - SHARE, S)
        old_last = variances[LAST][:, :S]
        doubled = roots[LAST - 1][:, few]
        weighed = terms[LAST - 1][:, HALF:]
        pooled = sbuf.tile([P, S], F32, name="pooled")
        look_up_variances(LAST)
        for part in (second, first):
            nc.scalar.activation(old_last[:, part], window(states[LAST], part), ACT.Copy)
        nc.scalar.activation(doubled, bank(LAST, few), ACT.Copy, scale=-2.0)
        root(LAST)
        for part in halves:
            square(LAST, part)
        nc.gpsimd.tensor_tensor(weighed[:, few], picked[LAST][:, few], doubled, ALU.mult)
        total(nc.gpsimd, LAST - 1, second)
        nc.vector.scalar_tensor_tensor(weighed[:, most], picked[LAST][:, most], -2.0, bank(LAST, most), ALU.mult, ALU.mult)
        scatter(LAST - 1, second)
        store(LAST - 1)
        for part in (few, most):
            nc.gpsimd.tensor_tensor(pooled[:, part], old_last[:, part], weighed[:, part], ALU.add)
        nc.vector.tensor_tensor(window(states[LAST], whole), stays[LAST], pooled[:], ALU.mult)
        store(LAST)
